import numpy as np
import ml_dtypes


def mxq(x, axis, fmt="e4m3"):
    dtype, down = {"e4m3": (ml_dtypes.float8_e4m3fn, 7), "e5m2": (ml_dtypes.float8_e5m2, 14)}[fmt]
    v = np.moveaxis(np.asarray(x, np.float32).astype(ml_dtypes.bfloat16).astype(np.float64), axis, -1)
    blocks = v.reshape(v.shape[:-1] + (-1, 32))
    amax = np.abs(blocks).max(-1, keepdims=True)
    byte = np.maximum(np.where(amax > 0, np.frexp(amax)[1] - 1 + 127, 0) - down, 1)
    scale = np.exp2(byte - 127.0)
    codes = (blocks / scale).astype(np.float32).astype(dtype).astype(np.float64)
    return np.moveaxis((codes * scale).reshape(v.shape), -1, axis)


WIDE = False


def mx_kscale(k):
    if not WIDE:
        return np.ones(k)
    levels = np.array([10, -10, 5, -5, 0])
    if k % 512:
        return np.exp2(np.random.permutation(np.resize(levels, k // 32))).repeat(32)
    a = np.empty((k // 512, 16))
    for p in range(k // 512):
        a[p, :8] = np.random.permutation(np.resize(levels, 8))
        for g in range(8):
            far = levels[np.abs(levels - a[p, g]) >= 10]
            a[p, g + 8] = far[np.random.randint(len(far))]
    return np.exp2(a.ravel()).repeat(32)


def f64(x):
    return np.asarray(x).astype(np.float64)


def striped(idx):
    return np.tile(np.asarray(idx).reshape(-1, 16).T, (8, 1)).astype(np.uint16)


def unstriped(offs):
    return offs[:16].T.reshape(-1).astype(np.int64)


E2M1 = np.array([0.0, 0.5, 1.0, 1.5, 2.0, 3.0, 4.0, 6.0, -0.0, -0.5, -1.0, -1.5, -2.0, -3.0, -4.0, -6.0])


def pack_weight(w, fmt):
    k, n = w.shape
    w = f64(np.asarray(w, np.float32).astype(ml_dtypes.bfloat16)).reshape(k // 32, 32, n)
    amax = np.abs(w).max(1)
    if fmt == "e4m3":
        byte = np.frexp(amax)[1] - 1 + 127 - 7
    else:
        mant, ex = np.frexp(amax / 6.0)
        byte = np.where(mant > 0.5, ex, ex - 1) + 127
    byte = np.clip(np.where(amax > 0, byte, 1), 1, 254)
    scaled = (w * np.exp2(127.0 - byte)[:, None, :]).reshape(k, n).astype(np.float32)
    by_word = np.ascontiguousarray(scaled.reshape(k // 512, 128, 4, n).transpose(0, 1, 3, 2))
    if fmt == "e4m3":
        words = by_word.astype(ml_dtypes.float8_e4m3fn).view(np.uint8)
    else:
        c = by_word.astype(ml_dtypes.float4_e2m1fn).view(np.uint8) & 0xF
        words = (c[..., 0::2] | (c[..., 1::2] << 4)).reshape(k // 512, 128, 2 * n)
    return np.ascontiguousarray(words), np.ascontiguousarray(byte.astype(np.uint8).reshape(k // 512, 16, n))


def unpack_weight(words, scales, fmt):
    g, _, n = scales.shape
    words = np.ascontiguousarray(words).reshape(g, 128, n, -1)
    if fmt == "e4m3":
        vals = words.view(ml_dtypes.float8_e4m3fn).astype(np.float64)
    else:
        nib = np.empty((g, 128, n, 4), np.uint8)
        nib[..., 0::2] = words & 0xF
        nib[..., 1::2] = words >> 4
        vals = E2M1[nib]
    vals = vals * np.repeat(np.exp2(scales.astype(np.float64) - 127.0), 8, axis=1)[..., None]
    return vals.transpose(0, 1, 3, 2).reshape(g * 512, n)


def softplus(v):
    return np.log(1.0 + np.exp(v))


B, N, T, D, NQ = 2, 512, 2048, 1024, 128


def setup_inputs():
    n = np.random.standard_normal
    jdx = np.random.permutation(1024)[:B * NQ]
    idx = np.random.permutation(T)[:B * N]
    s = mx_kscale(D)[:, None]
    kp = pack_weight(n((D, T)) / s, "e2m1")
    return {
        "qT": (n((D, 1024)) * s * (1.00 / np.sqrt(D))).astype(np.float32),
        "k_words": np.ascontiguousarray(kp[0].reshape(1, 2, 128, T, 2).transpose(0, 2, 3, 1, 4)).reshape(1, 128, T, 4),
        "k_scales": kp[1],
        "lq": np.tile(np.random.uniform(-1.0, 1.0, 2048), (128, 1)).astype(np.float32),
        "offq": striped(jdx),
        "offs": striped(idx),
    }


def reference(qT, k_words, k_scales, lq, offq, offs):
    jdx = unstriped(offq)
    idx = unstriped(offs)
    pick = lambda x, which: x[:, which].reshape(x.shape[0], B, -1).transpose(1, 0, 2)
    qg = mxq(pick(f64(qT), jdx), 1, "e4m3")
    k = unpack_weight(k_words.reshape(1, 128, T, 2, 2).transpose(0, 3, 1, 2, 4).reshape(2, 128, 2 * T), k_scales, "e2m1")
    kg = pick(k, idx)
    qq = qg
    a = qq.transpose(0, 2, 1) @ kg
    y = softplus(a - pick(f64(lq), idx)[:, :1, :])
    return y

@@ -1,0 +1,176 @@
+from contextlib import ExitStack
+
+import concourse.mybir as mybir
+from concourse.masks import make_identity
+
+F32 = mybir.dt.float32
+BF16 = mybir.dt.bfloat16
+I32 = mybir.dt.int32
+U32 = mybir.dt.uint32
+U16 = mybir.dt.uint16
+U8 = mybir.dt.uint8
+FP8X4 = mybir.dt.float8_e4m3fn_x4
+FP4X4 = mybir.dt.float4_e2m1fn_x4
+ACT = mybir.ActivationFunctionType
+ALU = mybir.AluOpType
+
+B, N, T, D, NQ, V = 2, 512, 2048, 1024, 128, 1024
+P = 128
+SLOTS = B * N
+QUERIES = B * NQ
+HALF = V // 2
+CHUNK = 256
+EXP_CAP = float(2**43)
+FLOPS = 2 * B * NQ * N * D
+BYTES = 4 * D * V + P * T * 4 + 2 * 16 * T + 4 * T + 2 * P * (16 + 64) + 4 * B * NQ * N
+
+
+def tile_attend_lq_sgns_topk_kernel(tc, qT, k_words, k_scales, lq, offq, offs, out):
+    nc = tc.nc
+    with ExitStack() as ctx:
+        keep = ctx.enter_context(tc.tile_pool(name="keep", bufs=1))
+        psum = ctx.enter_context(tc.psum_pool(name="psum", bufs=1))
+
+        slot_list = keep.tile([P, SLOTS // 16], U16, name="slot_list")
+        nc.sync.dma_start(slot_list[:], offs)
+
+        scale_pool = keep.tile([P, T // 4], I32, name="scale_pool")
+        scale_rows = k_scales.rearrange("o f t -> (o f) t").bitcast(I32)
+        nc.sync.dma_start(scale_pool[0:32, :], scale_rows)
+        for quad in range(1, 4):
+            nc.sync.dma_start(
+                scale_pool[32 * quad : 32 * quad + 32, :], scale_rows[4 * quad : 4 * quad + 4, :].partition_broadcast(8)
+            )
+
+        lq_pool = keep.tile([P, T], F32, name="lq_pool")
+        nc.sync.dma_start(lq_pool[P - 1 : P, :], lq[0:1, :])
+        nc.vector.memset(lq_pool[0 : P - 1, :], 0.0)
+
+        word_pool = keep.tile([P, T], I32, name="word_pool")
+        nc.sync.dma_start(word_pool[:], k_words[0].rearrange("p t b -> p (t b)").bitcast(I32))
+
+        query_list = keep.tile([P, QUERIES // 16], U16, name="query_list")
+
+        k_scale1 = keep.tile([P, SLOTS // 4], I32, name="k_scale1", align_bytes=64)
+        nc.vector.memset(k_scale1[:], 0)
+
+        ident = keep.tile([P, P], F32, name="ident")
+        make_identity(nc, ident[:])
+
+        q_rows = qT.rearrange("(o p r) n -> o p r n", o=2, r=4)
+        raw_pairs = []
+
+        def load_pair(pair):
+            o, r0 = pair // 2, 2 * (pair % 2)
+            halves = []
+            for h in range(2):
+                raw = keep.tile([P, 2, HALF], F32, name=f"raw_{pair}_{h}", tag=f"raw_{pair}_{h}")
+                nc.sync.dma_start(raw[:], q_rows[o, :, r0 : r0 + 2, h * HALF : (h + 1) * HALF])
+                halves.append(raw)
+            raw_pairs.append(halves)
+
+        load_pair(0)
+        load_pair(1)
+        nc.sync.dma_start(query_list[:], offq)
+
+        k_scale0 = keep.tile([P, SLOTS], U8, name="k_scale0", align_bytes=64)
+        nc.vector.tensor_copy(k_scale0[:], scale_pool[:].bitcast(U8).indirect(slot_list[:]))
+        for quad in range(4):
+            nc.sync.dma_start(k_scale1[32 * quad : 32 * quad + 4, :], k_scale0[16 + 4 * quad : 20 + 4 * quad, :].bitcast(I32))
+
+        load_pair(2)
+        load_pair(3)
+
+        lq_row = keep.tile([P, SLOTS], F32, name="lq_row")
+        nc.vector.tensor_copy(lq_row[:], lq_pool[:].indirect(slot_list[:]))
+
+        word_pairs = keep.tile([P, SLOTS], U32, name="word_pairs")
+        nc.vector.tensor_copy(word_pairs[:], word_pool[:].bitcast(U32).indirect(slot_list[:]))
+
+        k_codes = keep.tile([P, 2, SLOTS], U16, name="k_codes", align_bytes=64)
+        word_halves = word_pairs[:].bitcast(U16).rearrange("p (n o) -> p o n", o=2)
+        for o in range(2):
+            nc.vector.tensor_copy(k_codes[:, o, :], word_halves[:, o, :])
+
+        pair_pools = []
+
+        def cast_pair(pair):
+            pool_t = keep.tile([P, V, 2], BF16, name=f"pair_pool_{pair}")
+            for h in range(2):
+                nc.scalar.activation(
+                    pool_t[:, h * HALF : (h + 1) * HALF, :], raw_pairs[pair][h][:].rearrange("p r n -> p n r"), ACT.Copy
+                )
+            pair_pools.append(pool_t)
+
+        for pair in range(3):
+            cast_pair(pair)
+
+        lq_cols = keep.tile([P, SLOTS // P], F32, name="lq_cols", tag="raw_2_1")
+        for b in range(B):
+            turned = psum.tile([P, 4, P], F32, name=f"turned_{b}")
+            for j in range(4):
+                c = 4 * b + j
+                nc.tensor.transpose(turned[:, j, :], lq_row[:, c * P : (c + 1) * P], ident[:])
+            nc.scalar.activation(lq_cols[:, 4 * b : 4 * b + 4], turned[:, :, P - 1], ACT.Copy)
+        cast_pair(3)
+        lq_all = keep.tile([P, SLOTS], F32, name="lq_all", tag="raw_3_1")
+        for b in range(B):
+            spread = psum.tile([P, N], F32, name=f"spread_{b}")
+            for j in range(4):
+                c = 4 * b + j
+                nc.tensor.transpose(spread[:, j * P : (j + 1) * P], lq_cols[:, c : c + 1].to_broadcast([P, P]), ident[:])
+            nc.scalar.activation(lq_all[:, b * N : (b + 1) * N], spread[:], ACT.Copy)
+
+        q_grouped = [keep.tile([P, QUERIES, 4], BF16, name=f"q_grouped_{o}", align_bytes=64) for o in range(2)]
+        q_codes = [keep.tile([P, QUERIES], U32, name=f"q_codes_{o}", align_bytes=64) for o in range(2)]
+        q_scales = [keep.tile([P, QUERIES], U8, name=f"q_scales_{o}", align_bytes=64) for o in range(2)]
+
+        def gather_pair(pair, lo, hi):
+            words = q_grouped[pair // 2][:].rearrange("p n r -> p (n r)").bitcast(U32).rearrange("p (n h) -> p n h", h=2)
+            window = pair_pools[pair][:].rearrange("p n r -> p (n r)").bitcast(U32)
+            nc.vector.tensor_copy(words[:, lo:hi, pair % 2], window.indirect(query_list[:, lo // 16 : hi // 16]))
+
+        def quantize(o, lo, hi):
+            nc.vector.quantize_mx(
+                q_codes[o][:, lo:hi].bitcast(FP8X4),
+                q_scales[o][:, lo:hi],
+                q_grouped[o][:, lo:hi, :].rearrange("p n r -> p (n r)"),
+            )
+
+        gather_pair(0, 0, QUERIES)
+        gather_pair(1, 0, QUERIES)
+        gather_pair(2, 0, QUERIES)
+        quantize(0, 0, QUERIES)
+        for b in range(B):
+            gather_pair(3, b * NQ, (b + 1) * NQ)
+        for b in range(B):
+            quantize(1, b * NQ, (b + 1) * NQ)
+
+        k_scale = [k_scale0[:], k_scale1[:].bitcast(U8)]
+        scores = [psum.tile([P, N], F32, name=f"scores_{b}") for b in range(B)]
+        for o in range(2):
+            for b in range(B):
+                nc.tensor.matmul_mx(
+                    scores[b][:],
+                    lhsT=q_codes[o][:, b * NQ : (b + 1) * NQ].bitcast(FP8X4),
+                    lhsT_scale=q_scales[o][:, b * NQ : (b + 1) * NQ],
+                    rhs=k_codes[:, o, b * N : (b + 1) * N].bitcast(FP4X4),
+                    rhs_scale=k_scale[o][:, b * N : (b + 1) * N],
+                    start=(o == 0),
+                    stop=(o == 1),
+                )
+
+        diff = keep.tile([P, SLOTS], F32, name="diff")
+        grown = keep.tile([P, SLOTS], F32, name="grown")
+        capped = keep.tile([P, SLOTS], F32, name="capped")
+        logs = keep.tile([P, SLOTS], F32, name="logs")
+        result = keep.tile([P, SLOTS], F32, name="result")
+        chunks = [(lo // N, lo % N, slice(lo, lo + CHUNK)) for lo in range(0, SLOTS, CHUNK)]
+        for b, lo, cols in chunks:
+            nc.vector.tensor_tensor(diff[:, cols], scores[b][:, lo : lo + CHUNK], lq_all[:, cols], ALU.subtract)
+            nc.scalar.activation(grown[:, cols], diff[:, cols], ACT.Exp)
+        nc.vector.tensor_scalar_min(capped[:], grown[:], EXP_CAP)
+        for b, lo, cols in chunks:
+            nc.scalar.activation(logs[:, cols], capped[:, cols], ACT.Ln, bias=1.0)
+            nc.vector.tensor_tensor(result[:, cols], logs[:, cols], diff[:, cols], ALU.max)
+            nc.sync.dma_start(out[b, :, lo : lo + CHUNK], result[:, cols])

@@ -31,25 +31,22 @@ def tile_attend_lq_sgns_topk_kernel(tc, qT, k_words, k_scales, lq, offq, offs, o
         keep = ctx.enter_context(tc.tile_pool(name="keep", bufs=1))
         psum = ctx.enter_context(tc.psum_pool(name="psum", bufs=1))
 
+        scale_pool = keep.tile([P, T // 4], I32, name="scale_pool")
+        nc.vector.memset(scale_pool[:], 0)
+
         slot_list = keep.tile([P, SLOTS // 16], U16, name="slot_list")
         nc.sync.dma_start(slot_list[:], offs)
-
-        scale_pool = keep.tile([P, T // 4], I32, name="scale_pool")
-        scale_rows = k_scales.rearrange("o f t -> (o f) t").bitcast(I32)
-        nc.sync.dma_start(scale_pool[0:32, :], scale_rows)
-        for quad in range(1, 4):
-            nc.sync.dma_start(
-                scale_pool[32 * quad : 32 * quad + 32, :], scale_rows[4 * quad : 4 * quad + 4, :].partition_broadcast(8)
-            )
 
         lq_pool = keep.tile([P, T], F32, name="lq_pool")
         nc.sync.dma_start(lq_pool[P - 1 : P, :], lq[0:1, :])
         nc.vector.memset(lq_pool[0 : P - 1, :], 0.0)
 
+        scale_words = k_scales.bitcast(I32)
+        for quad in range(4):
+            nc.sync.dma_start(scale_pool[32 * quad : 32 * quad + 8, :], scale_words[:, 4 * quad : 4 * quad + 4, :])
+
         word_pool = keep.tile([P, T], I32, name="word_pool")
         nc.sync.dma_start(word_pool[:], k_words[0].rearrange("p t b -> p (t b)").bitcast(I32))
-
-        query_list = keep.tile([P, QUERIES // 16], U16, name="query_list")
 
         k_scale1 = keep.tile([P, SLOTS // 4], I32, name="k_scale1", align_bytes=64)
         nc.vector.memset(k_scale1[:], 0)
@@ -58,28 +55,20 @@ def tile_attend_lq_sgns_topk_kernel(tc, qT, k_words, k_scales, lq, offq, offs, o
         make_identity(nc, ident[:])
 
         q_rows = qT.rearrange("(o p r) n -> o p r n", o=2, r=4)
+        query_list = keep.tile([P, QUERIES // 16], U16, name="query_list")
         raw_pairs = []
-
-        def load_pair(pair):
+        for pair in range(3):
             o, r0 = pair // 2, 2 * (pair % 2)
-            halves = []
-            for h in range(2):
-                raw = keep.tile([P, 2, HALF], F32, name=f"raw_{pair}_{h}", tag=f"raw_{pair}_{h}")
-                nc.sync.dma_start(raw[:], q_rows[o, :, r0 : r0 + 2, h * HALF : (h + 1) * HALF])
-                halves.append(raw)
-            raw_pairs.append(halves)
-
-        load_pair(0)
-        load_pair(1)
-        nc.sync.dma_start(query_list[:], offq)
-
-        k_scale0 = keep.tile([P, SLOTS], U8, name="k_scale0", align_bytes=64)
-        nc.vector.tensor_copy(k_scale0[:], scale_pool[:].bitcast(U8).indirect(slot_list[:]))
-        for quad in range(4):
-            nc.sync.dma_start(k_scale1[32 * quad : 32 * quad + 4, :], k_scale0[16 + 4 * quad : 20 + 4 * quad, :].bitcast(I32))
-
-        load_pair(2)
-        load_pair(3)
+            raw = keep.tile([P, 2, V], F32, name=f"raw_{pair}", tag=f"raw_{pair}")
+            nc.sync.dma_start(raw[:], q_rows[o, :, r0 : r0 + 2, :])
+            raw_pairs.append(raw)
+            if pair == 0:
+                nc.sync.dma_start(query_list[:], offq)
+        raw_rows = []
+        for r in (2, 3):
+            raw = keep.tile([P, V], F32, name=f"raw_row_{r}")
+            nc.sync.dma_start(raw[:], q_rows[1, :, r, :])
+            raw_rows.append(raw)
 
         lq_row = keep.tile([P, SLOTS], F32, name="lq_row")
         nc.vector.tensor_copy(lq_row[:], lq_pool[:].indirect(slot_list[:]))
@@ -87,33 +76,31 @@ def tile_attend_lq_sgns_topk_kernel(tc, qT, k_words, k_scales, lq, offq, offs, o
         word_pairs = keep.tile([P, SLOTS], U32, name="word_pairs")
         nc.vector.tensor_copy(word_pairs[:], word_pool[:].bitcast(U32).indirect(slot_list[:]))
 
+        k_scale0 = keep.tile([P, SLOTS], U8, name="k_scale0", align_bytes=64)
+        nc.vector.tensor_copy(k_scale0[:], scale_pool[:].bitcast(U8).indirect(slot_list[:]))
+        for quad in range(4):
+            nc.sync.dma_start(k_scale1[32 * quad : 32 * quad + 4, :], k_scale0[32 * quad + 4 : 32 * quad + 8, :].bitcast(I32))
+
         k_codes = keep.tile([P, 2, SLOTS], U16, name="k_codes", align_bytes=64)
         word_halves = word_pairs[:].bitcast(U16).rearrange("p (n o) -> p o n", o=2)
         for o in range(2):
             nc.vector.tensor_copy(k_codes[:, o, :], word_halves[:, o, :])
 
-        pair_pools = []
-
-        def cast_pair(pair):
-            pool_t = keep.tile([P, V, 2], BF16, name=f"pair_pool_{pair}")
-            for h in range(2):
-                nc.scalar.activation(
-                    pool_t[:, h * HALF : (h + 1) * HALF, :], raw_pairs[pair][h][:].rearrange("p r n -> p n r"), ACT.Copy
-                )
-            pair_pools.append(pool_t)
-
-        for pair in range(3):
-            cast_pair(pair)
-
-        lq_cols = keep.tile([P, SLOTS // P], F32, name="lq_cols", tag="raw_2_1")
+        lq_cols = keep.tile([P, SLOTS // P], F32, name="lq_cols")
         for b in range(B):
             turned = psum.tile([P, 4, P], F32, name=f"turned_{b}")
             for j in range(4):
                 c = 4 * b + j
                 nc.tensor.transpose(turned[:, j, :], lq_row[:, c * P : (c + 1) * P], ident[:])
             nc.scalar.activation(lq_cols[:, 4 * b : 4 * b + 4], turned[:, :, P - 1], ACT.Copy)
-        cast_pair(3)
-        lq_all = keep.tile([P, SLOTS], F32, name="lq_all", tag="raw_3_1")
+
+        pair_pools = []
+        for pair in range(3):
+            pool_t = keep.tile([P, V, 2], BF16, name=f"pair_pool_{pair}")
+            nc.scalar.activation(pool_t[:], raw_pairs[pair][:].rearrange("p r n -> p n r"), ACT.Copy)
+            pair_pools.append(pool_t)
+
+        lq_all = keep.tile([P, SLOTS], F32, name="lq_all", tag="raw_2")
         for b in range(B):
             spread = psum.tile([P, N], F32, name=f"spread_{b}")
             for j in range(4):
@@ -137,14 +124,19 @@ def tile_attend_lq_sgns_topk_kernel(tc, qT, k_words, k_scales, lq, offq, offs, o
                 q_grouped[o][:, lo:hi, :].rearrange("p n r -> p (n r)"),
             )
 
+        def gather_row(r, lo, hi):
+            nc.vector.tensor_copy(q_grouped[1][:, lo:hi, r], raw_rows[r - 2][:].indirect(query_list[:, lo // 16 : hi // 16]))
+
         gather_pair(0, 0, QUERIES)
         gather_pair(1, 0, QUERIES)
-        gather_pair(2, 0, QUERIES)
+        gather_row(2, 0, QUERIES)
         quantize(0, 0, QUERIES)
-        for b in range(B):
-            gather_pair(3, b * NQ, (b + 1) * NQ)
-        for b in range(B):
-            quantize(1, b * NQ, (b + 1) * NQ)
+        gather_row(3, 0, NQ)
+        gather_pair(2, 0, NQ)
+        gather_row(3, NQ, QUERIES)
+        quantize(1, 0, NQ)
+        gather_pair(2, NQ, QUERIES)
+        quantize(1, NQ, QUERIES)
 
         k_scale = [k_scale0[:], k_scale1[:].bitcast(U8)]
         scores = [psum.tile([P, N], F32, name=f"scores_{b}") for b in range(B)]
@@ -170,7 +162,8 @@ def tile_attend_lq_sgns_topk_kernel(tc, qT, k_words, k_scales, lq, offq, offs, o
             nc.vector.tensor_tensor(diff[:, cols], scores[b][:, lo : lo + CHUNK], lq_all[:, cols], ALU.subtract)
             nc.scalar.activation(grown[:, cols], diff[:, cols], ACT.Exp)
         nc.vector.tensor_scalar_min(capped[:], grown[:], EXP_CAP)
-        for b, lo, cols in chunks:
+        for lo, hi in ((0, 256), (256, 512), (512, 768), (768, 896), (896, 1024)):
+            cols = slice(lo, hi)
             nc.scalar.activation(logs[:, cols], capped[:, cols], ACT.Ln, bias=1.0)
             nc.vector.tensor_tensor(result[:, cols], logs[:, cols], diff[:, cols], ALU.max)
-            nc.sync.dma_start(out[b, :, lo : lo + CHUNK], result[:, cols])
+            nc.sync.dma_start(out[lo // N, :, lo % N : lo % N + hi - lo], result[:, cols])

@@ -31,7 +31,7 @@ def tile_attend_lq_sgns_topk_kernel(tc, qT, k_words, k_scales, lq, offq, offs, o
         keep = ctx.enter_context(tc.tile_pool(name="keep", bufs=1))
         psum = ctx.enter_context(tc.psum_pool(name="psum", bufs=1))
 
-        scale_pool = keep.tile([P, T // 4], I32, name="scale_pool")
+        scale_pool = keep.tile([P, T // 4], I32, name="scale_pool", tag="scales_then_rows")
         nc.vector.memset(scale_pool[:], 0)
 
         slot_list = keep.tile([P, SLOTS // 16], U16, name="slot_list")
@@ -45,46 +45,55 @@ def tile_attend_lq_sgns_topk_kernel(tc, qT, k_words, k_scales, lq, offq, offs, o
         for quad in range(4):
             nc.sync.dma_start(scale_pool[32 * quad : 32 * quad + 8, :], scale_words[:, 4 * quad : 4 * quad + 4, :])
 
-        word_pool = keep.tile([P, T], I32, name="word_pool")
-        nc.sync.dma_start(word_pool[:], k_words[0].rearrange("p t b -> p (t b)").bitcast(I32))
-
         k_scale1 = keep.tile([P, SLOTS // 4], I32, name="k_scale1", align_bytes=64)
-        nc.vector.memset(k_scale1[:], 0)
+        nc.gpsimd.memset(k_scale1[:], 0)
 
         ident = keep.tile([P, P], F32, name="ident")
         make_identity(nc, ident[:])
 
         q_rows = qT.rearrange("(o p r) n -> o p r n", o=2, r=4)
         query_list = keep.tile([P, QUERIES // 16], U16, name="query_list")
-        raw_pairs = []
-        for pair in range(3):
-            o, r0 = pair // 2, 2 * (pair % 2)
-            raw = keep.tile([P, 2, V], F32, name=f"raw_{pair}", tag=f"raw_{pair}")
-            nc.sync.dma_start(raw[:], q_rows[o, :, r0 : r0 + 2, :])
-            raw_pairs.append(raw)
-            if pair == 0:
+        word_pool = keep.tile([P, T], I32, name="word_pool")
+        raw0 = [keep.tile([P, V], F32, name=f"raw0_{r}") for r in range(4)]
+        for r in range(4):
+            nc.sync.dma_start(raw0[r][:], q_rows[0, :, r, :])
+            if r == 1:
                 nc.sync.dma_start(query_list[:], offq)
-        raw_rows = []
-        for r in (2, 3):
-            raw = keep.tile([P, V], F32, name=f"raw_row_{r}")
-            nc.sync.dma_start(raw[:], q_rows[1, :, r, :])
-            raw_rows.append(raw)
+                nc.sync.dma_start(word_pool[:], k_words[0].rearrange("p t b -> p (t b)").bitcast(I32))
+        raw_pair = keep.tile([P, 2, V], F32, name="raw_pair", tag="pair_then_lq")
+        nc.sync.dma_start(raw_pair[:], q_rows[1, :, 0:2, :])
 
         lq_row = keep.tile([P, SLOTS], F32, name="lq_row")
         nc.vector.tensor_copy(lq_row[:], lq_pool[:].indirect(slot_list[:]))
-
-        word_pairs = keep.tile([P, SLOTS], U32, name="word_pairs")
-        nc.vector.tensor_copy(word_pairs[:], word_pool[:].bitcast(U32).indirect(slot_list[:]))
 
         k_scale0 = keep.tile([P, SLOTS], U8, name="k_scale0", align_bytes=64)
         nc.vector.tensor_copy(k_scale0[:], scale_pool[:].bitcast(U8).indirect(slot_list[:]))
         for quad in range(4):
             nc.sync.dma_start(k_scale1[32 * quad : 32 * quad + 4, :], k_scale0[32 * quad + 4 : 32 * quad + 8, :].bitcast(I32))
 
+        raw_last = keep.tile([P, 2, V], F32, name="raw_last", tag="scales_then_rows")
+        for r in range(2):
+            nc.sync.dma_start(raw_last[:, r, :], q_rows[1, :, 2 + r, :])
+
+        word_pairs = keep.tile([P, SLOTS], U32, name="word_pairs")
+        nc.vector.tensor_copy(word_pairs[:], word_pool[:].bitcast(U32).indirect(slot_list[:]))
+
         k_codes = keep.tile([P, 2, SLOTS], U16, name="k_codes", align_bytes=64)
         word_halves = word_pairs[:].bitcast(U16).rearrange("p (n o) -> p o n", o=2)
         for o in range(2):
             nc.vector.tensor_copy(k_codes[:, o, :], word_halves[:, o, :])
+
+        q_grouped = [keep.tile([P, QUERIES, 4], BF16, name=f"q_grouped_{o}", align_bytes=64) for o in range(2)]
+        q_codes = [keep.tile([P, QUERIES], U32, name=f"q_codes_{o}", align_bytes=64) for o in range(2)]
+        q_scales = [keep.tile([P, QUERIES], U8, name=f"q_scales_{o}", align_bytes=64) for o in range(2)]
+
+        def scalar_row(r):
+            rounded = keep.tile([P, V], BF16, name=f"rounded_{r}")
+            nc.scalar.activation(rounded[:], raw0[r][:], ACT.Copy)
+            nc.scalar.activation(q_grouped[0][:, :, r], rounded[:].indirect(query_list[:]), ACT.Copy)
+
+        scalar_row(0)
+        scalar_row(1)
 
         lq_cols = keep.tile([P, SLOTS // P], F32, name="lq_cols")
         for b in range(B):
@@ -94,13 +103,13 @@ def tile_attend_lq_sgns_topk_kernel(tc, qT, k_words, k_scales, lq, offq, offs, o
                 nc.tensor.transpose(turned[:, j, :], lq_row[:, c * P : (c + 1) * P], ident[:])
             nc.scalar.activation(lq_cols[:, 4 * b : 4 * b + 4], turned[:, :, P - 1], ACT.Copy)
 
-        pair_pools = []
-        for pair in range(3):
-            pool_t = keep.tile([P, V, 2], BF16, name=f"pair_pool_{pair}")
-            nc.scalar.activation(pool_t[:], raw_pairs[pair][:].rearrange("p r n -> p n r"), ACT.Copy)
-            pair_pools.append(pool_t)
+        scalar_row(2)
+        scalar_row(3)
 
-        lq_all = keep.tile([P, SLOTS], F32, name="lq_all", tag="raw_2")
+        pair_pool = keep.tile([P, V, 2], BF16, name="pair_pool")
+        nc.scalar.activation(pair_pool[:], raw_pair[:].rearrange("p r n -> p n r"), ACT.Copy)
+
+        lq_all = keep.tile([P, SLOTS], F32, name="lq_all", tag="pair_then_lq")
         for b in range(B):
             spread = psum.tile([P, N], F32, name=f"spread_{b}")
             for j in range(4):
@@ -108,14 +117,13 @@ def tile_attend_lq_sgns_topk_kernel(tc, qT, k_words, k_scales, lq, offq, offs, o
                 nc.tensor.transpose(spread[:, j * P : (j + 1) * P], lq_cols[:, c : c + 1].to_broadcast([P, P]), ident[:])
             nc.scalar.activation(lq_all[:, b * N : (b + 1) * N], spread[:], ACT.Copy)
 
-        q_grouped = [keep.tile([P, QUERIES, 4], BF16, name=f"q_grouped_{o}", align_bytes=64) for o in range(2)]
-        q_codes = [keep.tile([P, QUERIES], U32, name=f"q_codes_{o}", align_bytes=64) for o in range(2)]
-        q_scales = [keep.tile([P, QUERIES], U8, name=f"q_scales_{o}", align_bytes=64) for o in range(2)]
+        def gather_pair(lo, hi):
+            words = q_grouped[1][:].rearrange("p n r -> p (n r)").bitcast(U32).rearrange("p (n h) -> p n h", h=2)
+            window = pair_pool[:].rearrange("p n r -> p (n r)").bitcast(U32)
+            nc.vector.tensor_copy(words[:, lo:hi, 0], window.indirect(query_list[:, lo // 16 : hi // 16]))
 
-        def gather_pair(pair, lo, hi):
-            words = q_grouped[pair // 2][:].rearrange("p n r -> p (n r)").bitcast(U32).rearrange("p (n h) -> p n h", h=2)
-            window = pair_pools[pair][:].rearrange("p n r -> p (n r)").bitcast(U32)
-            nc.vector.tensor_copy(words[:, lo:hi, pair % 2], window.indirect(query_list[:, lo // 16 : hi // 16]))
+        def gather_row(r, lo, hi):
+            nc.vector.tensor_copy(q_grouped[1][:, lo:hi, r], raw_last[:, r - 2, :].indirect(query_list[:, lo // 16 : hi // 16]))
 
         def quantize(o, lo, hi):
             nc.vector.quantize_mx(
@@ -124,18 +132,13 @@ def tile_attend_lq_sgns_topk_kernel(tc, qT, k_words, k_scales, lq, offq, offs, o
                 q_grouped[o][:, lo:hi, :].rearrange("p n r -> p (n r)"),
             )
 
-        def gather_row(r, lo, hi):
-            nc.vector.tensor_copy(q_grouped[1][:, lo:hi, r], raw_rows[r - 2][:].indirect(query_list[:, lo // 16 : hi // 16]))
-
-        gather_pair(0, 0, QUERIES)
-        gather_pair(1, 0, QUERIES)
-        gather_row(2, 0, QUERIES)
         quantize(0, 0, QUERIES)
+        gather_row(2, 0, QUERIES)
         gather_row(3, 0, NQ)
-        gather_pair(2, 0, NQ)
+        gather_pair(0, NQ)
         gather_row(3, NQ, QUERIES)
         quantize(1, 0, NQ)
-        gather_pair(2, NQ, QUERIES)
+        gather_pair(NQ, QUERIES)
         quantize(1, NQ, QUERIES)
 
         k_scale = [k_scale0[:], k_scale1[:].bitcast(U8)]

@@ -31,7 +31,7 @@ def tile_attend_lq_sgns_topk_kernel(tc, qT, k_words, k_scales, lq, offq, offs, o
         keep = ctx.enter_context(tc.tile_pool(name="keep", bufs=1))
         psum = ctx.enter_context(tc.psum_pool(name="psum", bufs=1))
 
-        scale_pool = keep.tile([P, T // 4], I32, name="scale_pool", tag="scales_then_rows")
+        scale_pool = keep.tile([P, T // 4], I32, name="scale_pool")
         nc.vector.memset(scale_pool[:], 0)
 
         slot_list = keep.tile([P, SLOTS // 16], U16, name="slot_list")
@@ -52,16 +52,20 @@ def tile_attend_lq_sgns_topk_kernel(tc, qT, k_words, k_scales, lq, offq, offs, o
         make_identity(nc, ident[:])
 
         q_rows = qT.rearrange("(o p r) n -> o p r n", o=2, r=4)
+
+        def load_row(o, r, tag):
+            raw = keep.tile([P, V], F32, name=f"raw_{o}_{r}", tag=tag, align_bytes=64)
+            nc.sync.dma_start(raw[:], q_rows[o, :, r, :])
+            return raw[:]
+
+        raw0 = [load_row(0, 0, "row_0"), load_row(0, 1, "first_then_cols")]
         query_list = keep.tile([P, QUERIES // 16], U16, name="query_list")
+        nc.sync.dma_start(query_list[:], offq)
         word_pool = keep.tile([P, T], I32, name="word_pool")
-        raw0 = [keep.tile([P, V], F32, name=f"raw0_{r}") for r in range(4)]
-        for r in range(4):
-            nc.sync.dma_start(raw0[r][:], q_rows[0, :, r, :])
-            if r == 1:
-                nc.sync.dma_start(query_list[:], offq)
-                nc.sync.dma_start(word_pool[:], k_words[0].rearrange("p t b -> p (t b)").bitcast(I32))
-        raw_pair = keep.tile([P, 2, V], F32, name="raw_pair", tag="pair_then_lq")
-        nc.sync.dma_start(raw_pair[:], q_rows[1, :, 0:2, :])
+        nc.sync.dma_start(word_pool[:], k_words[0].rearrange("p t b -> p (t b)").bitcast(I32))
+        raw0.append(load_row(0, 2, "row_2"))
+        raw0.append(load_row(0, 3, "row_then_lq"))
+        raw1 = [load_row(1, r, f"row_{4 + r}") for r in range(4)]
 
         lq_row = keep.tile([P, SLOTS], F32, name="lq_row")
         nc.vector.tensor_copy(lq_row[:], lq_pool[:].indirect(slot_list[:]))
@@ -70,10 +74,6 @@ def tile_attend_lq_sgns_topk_kernel(tc, qT, k_words, k_scales, lq, offq, offs, o
         nc.vector.tensor_copy(k_scale0[:], scale_pool[:].bitcast(U8).indirect(slot_list[:]))
         for quad in range(4):
             nc.sync.dma_start(k_scale1[32 * quad : 32 * quad + 4, :], k_scale0[32 * quad + 4 : 32 * quad + 8, :].bitcast(I32))
-
-        raw_last = keep.tile([P, 2, V], F32, name="raw_last", tag="scales_then_rows")
-        for r in range(2):
-            nc.sync.dma_start(raw_last[:, r, :], q_rows[1, :, 2 + r, :])
 
         word_pairs = keep.tile([P, SLOTS], U32, name="word_pairs")
         nc.vector.tensor_copy(word_pairs[:], word_pool[:].bitcast(U32).indirect(slot_list[:]))
@@ -84,20 +84,19 @@ def tile_attend_lq_sgns_topk_kernel(tc, qT, k_words, k_scales, lq, offq, offs, o
             nc.vector.tensor_copy(k_codes[:, o, :], word_halves[:, o, :])
 
         q_grouped = [keep.tile([P, QUERIES, 4], BF16, name=f"q_grouped_{o}", align_bytes=64) for o in range(2)]
-        q_codes = [keep.tile([P, QUERIES], U32, name=f"q_codes_{o}", align_bytes=64) for o in range(2)]
         q_scales = [keep.tile([P, QUERIES], U8, name=f"q_scales_{o}", align_bytes=64) for o in range(2)]
 
         def scalar_row(r):
             rounded = keep.tile([P, V], BF16, name=f"rounded_{r}")
-            nc.scalar.activation(rounded[:], raw0[r][:], ACT.Copy)
+            nc.scalar.activation(rounded[:], raw0[r], ACT.Copy)
             nc.scalar.activation(q_grouped[0][:, :, r], rounded[:].indirect(query_list[:]), ACT.Copy)
 
         scalar_row(0)
         scalar_row(1)
 
-        lq_cols = keep.tile([P, SLOTS // P], F32, name="lq_cols")
+        lq_cols = keep.tile([P, SLOTS // P], F32, name="lq_cols", tag="first_then_cols", align_bytes=64)
         for b in range(B):
-            turned = psum.tile([P, 4, P], F32, name=f"turned_{b}")
+            turned = psum.tile([P, 4, P], F32, name=f"turned_{b}", tag=f"bank_{4 + b}")
             for j in range(4):
                 c = 4 * b + j
                 nc.tensor.transpose(turned[:, j, :], lq_row[:, c * P : (c + 1) * P], ident[:])
@@ -106,24 +105,16 @@ def tile_attend_lq_sgns_topk_kernel(tc, qT, k_words, k_scales, lq, offq, offs, o
         scalar_row(2)
         scalar_row(3)
 
-        pair_pool = keep.tile([P, V, 2], BF16, name="pair_pool")
-        nc.scalar.activation(pair_pool[:], raw_pair[:].rearrange("p r n -> p n r"), ACT.Copy)
-
-        lq_all = keep.tile([P, SLOTS], F32, name="lq_all", tag="pair_then_lq")
+        lq_all = keep.tile([P, SLOTS], F32, name="lq_all", tag="row_then_lq", align_bytes=64)
         for b in range(B):
-            spread = psum.tile([P, N], F32, name=f"spread_{b}")
+            spread = psum.tile([P, N], F32, name=f"spread_{b}", tag=f"bank_{6 + b}")
             for j in range(4):
                 c = 4 * b + j
                 nc.tensor.transpose(spread[:, j * P : (j + 1) * P], lq_cols[:, c : c + 1].to_broadcast([P, P]), ident[:])
             nc.scalar.activation(lq_all[:, b * N : (b + 1) * N], spread[:], ACT.Copy)
 
-        def gather_pair(lo, hi):
-            words = q_grouped[1][:].rearrange("p n r -> p (n r)").bitcast(U32).rearrange("p (n h) -> p n h", h=2)
-            window = pair_pool[:].rearrange("p n r -> p (n r)").bitcast(U32)
-            nc.vector.tensor_copy(words[:, lo:hi, 0], window.indirect(query_list[:, lo // 16 : hi // 16]))
-
         def gather_row(r, lo, hi):
-            nc.vector.tensor_copy(q_grouped[1][:, lo:hi, r], raw_last[:, r - 2, :].indirect(query_list[:, lo // 16 : hi // 16]))
+            nc.vector.tensor_copy(q_grouped[1][:, lo:hi, r], raw1[r].indirect(query_list[:, lo // 16 : hi // 16]))
 
         def quantize(o, lo, hi):
             nc.vector.quantize_mx(
@@ -132,25 +123,29 @@ def tile_attend_lq_sgns_topk_kernel(tc, qT, k_words, k_scales, lq, offq, offs, o
                 q_grouped[o][:, lo:hi, :].rearrange("p n r -> p (n r)"),
             )
 
+        for r in range(3):
+            gather_row(r, 0, QUERIES)
+        q_codes = [
+            keep.tile([P, QUERIES], U32, name="q_codes_0", tag="row_6", align_bytes=64),
+            keep.tile([P, QUERIES], U32, name="q_codes_1", align_bytes=64),
+        ]
         quantize(0, 0, QUERIES)
-        gather_row(2, 0, QUERIES)
-        gather_row(3, 0, NQ)
-        gather_pair(0, NQ)
-        gather_row(3, NQ, QUERIES)
-        quantize(1, 0, NQ)
-        gather_pair(NQ, QUERIES)
-        quantize(1, NQ, QUERIES)
+        for b in range(B):
+            gather_row(3, b * NQ, (b + 1) * NQ)
+        for b in range(B):
+            quantize(1, b * NQ, (b + 1) * NQ)
 
         k_scale = [k_scale0[:], k_scale1[:].bitcast(U8)]
-        scores = [psum.tile([P, N], F32, name=f"scores_{b}") for b in range(B)]
+        scores = [psum.tile([P, P], F32, name=f"scores_{c}", tag=f"bank_{c}") for c in range(SLOTS // P)]
         for o in range(2):
-            for b in range(B):
+            for c in range(SLOTS // P):
+                b = c * P // N
                 nc.tensor.matmul_mx(
-                    scores[b][:],
+                    scores[c][:],
                     lhsT=q_codes[o][:, b * NQ : (b + 1) * NQ].bitcast(FP8X4),
                     lhsT_scale=q_scales[o][:, b * NQ : (b + 1) * NQ],
-                    rhs=k_codes[:, o, b * N : (b + 1) * N].bitcast(FP4X4),
-                    rhs_scale=k_scale[o][:, b * N : (b + 1) * N],
+                    rhs=k_codes[:, o, c * P : (c + 1) * P].bitcast(FP4X4),
+                    rhs_scale=k_scale[o][:, c * P : (c + 1) * P],
                     start=(o == 0),
                     stop=(o == 1),
                 )
@@ -160,10 +155,11 @@ def tile_attend_lq_sgns_topk_kernel(tc, qT, k_words, k_scales, lq, offq, offs, o
         capped = keep.tile([P, SLOTS], F32, name="capped")
         logs = keep.tile([P, SLOTS], F32, name="logs")
         result = keep.tile([P, SLOTS], F32, name="result")
-        chunks = [(lo // N, lo % N, slice(lo, lo + CHUNK)) for lo in range(0, SLOTS, CHUNK)]
-        for b, lo, cols in chunks:
-            nc.vector.tensor_tensor(diff[:, cols], scores[b][:, lo : lo + CHUNK], lq_all[:, cols], ALU.subtract)
-            nc.scalar.activation(grown[:, cols], diff[:, cols], ACT.Exp)
+        for lo, hi in ((0, 128), (128, 384), (384, 640), (640, 896), (896, 1024)):
+            for c in range(lo // P, hi // P):
+                cols = slice(c * P, (c + 1) * P)
+                nc.vector.tensor_tensor(diff[:, cols], scores[c][:], lq_all[:, cols], ALU.subtract)
+            nc.scalar.activation(grown[:, lo:hi], diff[:, lo:hi], ACT.Exp)
         nc.vector.tensor_scalar_min(capped[:], grown[:], EXP_CAP)
         for lo, hi in ((0, 256), (256, 512), (512, 768), (768, 896), (896, 1024)):
             cols = slice(lo, hi)

@@ -41,9 +41,10 @@ def tile_attend_lq_sgns_topk_kernel(tc, qT, k_words, k_scales, lq, offq, offs, o
         nc.sync.dma_start(lq_pool[P - 1 : P, :], lq[0:1, :])
         nc.vector.memset(lq_pool[0 : P - 1, :], 0.0)
 
-        scale_words = k_scales.bitcast(I32)
-        for quad in range(4):
-            nc.sync.dma_start(scale_pool[32 * quad : 32 * quad + 8, :], scale_words[:, 4 * quad : 4 * quad + 4, :])
+        scale_rows = k_scales.rearrange("o f t -> (o f) t").bitcast(I32)
+        nc.sync.dma_start(scale_pool[0:32, :], scale_rows)
+        for quad in range(1, 4):
+            nc.sync.dma_start(scale_pool[32 * quad : 32 * quad + 4, :], scale_rows[4 * quad : 4 * quad + 4, :])
 
         k_scale1 = keep.tile([P, SLOTS // 4], I32, name="k_scale1", align_bytes=64)
         nc.gpsimd.memset(k_scale1[:], 0)
@@ -73,7 +74,7 @@ def tile_attend_lq_sgns_topk_kernel(tc, qT, k_words, k_scales, lq, offq, offs, o
         k_scale0 = keep.tile([P, SLOTS], U8, name="k_scale0", align_bytes=64)
         nc.vector.tensor_copy(k_scale0[:], scale_pool[:].bitcast(U8).indirect(slot_list[:]))
         for quad in range(4):
-            nc.sync.dma_start(k_scale1[32 * quad : 32 * quad + 4, :], k_scale0[32 * quad + 4 : 32 * quad + 8, :].bitcast(I32))
+            nc.sync.dma_start(k_scale1[32 * quad : 32 * quad + 4, :], k_scale0[16 + 4 * quad : 20 + 4 * quad, :].bitcast(I32))
 
         word_pairs = keep.tile([P, SLOTS], U32, name="word_pairs")
         nc.vector.tensor_copy(word_pairs[:], word_pool[:].bitcast(U32).indirect(slot_list[:]))

@@ -32,22 +32,22 @@ def tile_attend_lq_sgns_topk_kernel(tc, qT, k_words, k_scales, lq, offq, offs, o
         psum = ctx.enter_context(tc.psum_pool(name="psum", bufs=1))
 
         scale_pool = keep.tile([P, T // 4], I32, name="scale_pool")
-        nc.vector.memset(scale_pool[:], 0)
+        nc.gpsimd.memset(scale_pool[32:64, :], 0)
+        nc.gpsimd.memset(scale_pool[64:128, :], 0)
 
         slot_list = keep.tile([P, SLOTS // 16], U16, name="slot_list")
         nc.sync.dma_start(slot_list[:], offs)
+
+        scale_rows = k_scales.rearrange("o f t -> (o f) t").bitcast(I32)
+        nc.sync.dma_start(scale_pool[0:32, :], scale_rows)
 
         lq_pool = keep.tile([P, T], F32, name="lq_pool")
         nc.sync.dma_start(lq_pool[P - 1 : P, :], lq[0:1, :])
         nc.vector.memset(lq_pool[0 : P - 1, :], 0.0)
 
-        scale_rows = k_scales.rearrange("o f t -> (o f) t").bitcast(I32)
-        nc.sync.dma_start(scale_pool[0:32, :], scale_rows)
-        for quad in range(1, 4):
-            nc.sync.dma_start(scale_pool[32 * quad : 32 * quad + 4, :], scale_rows[4 * quad : 4 * quad + 4, :])
-
-        k_scale1 = keep.tile([P, SLOTS // 4], I32, name="k_scale1", align_bytes=64)
-        nc.gpsimd.memset(k_scale1[:], 0)
+        k_planes = [keep.tile([P, SLOTS // 4], I32, name=f"k_plane_{o}", align_bytes=64) for o in range(2)]
+        for o in range(2):
+            nc.vector.memset(k_planes[o][:], 0)
 
         ident = keep.tile([P, P], F32, name="ident")
         make_identity(nc, ident[:])
@@ -64,25 +64,32 @@ def tile_attend_lq_sgns_topk_kernel(tc, qT, k_words, k_scales, lq, offq, offs, o
         nc.sync.dma_start(query_list[:], offq)
         word_pool = keep.tile([P, T], I32, name="word_pool")
         nc.sync.dma_start(word_pool[:], k_words[0].rearrange("p t b -> p (t b)").bitcast(I32))
+
+        def load_pair(o, r, tag):
+            raw = keep.tile([P, 2, V], F32, name=f"raw_{o}_{r}", tag=tag, align_bytes=64)
+            nc.sync.dma_start(raw[:], q_rows[o, :, r : r + 2, :])
+            return [raw[:, 0, :], raw[:, 1, :]]
+
         raw0.append(load_row(0, 2, "row_2"))
         raw0.append(load_row(0, 3, "row_then_lq"))
-        raw1 = [load_row(1, r, f"row_{4 + r}") for r in range(4)]
+        raw1 = load_pair(1, 0, "row_4") + [load_row(1, r, f"row_{4 + r}") for r in range(2, 4)]
+
+        scale_picked = keep.tile([P, SLOTS], U8, name="scale_picked", align_bytes=64)
+        nc.vector.tensor_copy(scale_picked[:], scale_pool[:].bitcast(U8).indirect(slot_list[:]))
+        for o, queue in enumerate((nc.gpsimd, nc.sync)):
+            for quad in range(4):
+                row = 16 * o + 4 * quad
+                queue.dma_start(k_planes[o][32 * quad : 32 * quad + 4, :], scale_picked[row : row + 4, :].bitcast(I32))
 
         lq_row = keep.tile([P, SLOTS], F32, name="lq_row")
         nc.vector.tensor_copy(lq_row[:], lq_pool[:].indirect(slot_list[:]))
-
-        k_scale0 = keep.tile([P, SLOTS], U8, name="k_scale0", align_bytes=64)
-        nc.vector.tensor_copy(k_scale0[:], scale_pool[:].bitcast(U8).indirect(slot_list[:]))
-        for quad in range(4):
-            nc.sync.dma_start(k_scale1[32 * quad : 32 * quad + 4, :], k_scale0[16 + 4 * quad : 20 + 4 * quad, :].bitcast(I32))
 
         word_pairs = keep.tile([P, SLOTS], U32, name="word_pairs")
         nc.vector.tensor_copy(word_pairs[:], word_pool[:].bitcast(U32).indirect(slot_list[:]))
 
         k_codes = keep.tile([P, 2, SLOTS], U16, name="k_codes", align_bytes=64)
         word_halves = word_pairs[:].bitcast(U16).rearrange("p (n o) -> p o n", o=2)
-        for o in range(2):
-            nc.vector.tensor_copy(k_codes[:, o, :], word_halves[:, o, :])
+        nc.vector.tensor_copy(k_codes[:], word_halves)
 
         q_grouped = [keep.tile([P, QUERIES, 4], BF16, name=f"q_grouped_{o}", align_bytes=64) for o in range(2)]
         q_scales = [keep.tile([P, QUERIES], U8, name=f"q_scales_{o}", align_bytes=64) for o in range(2)]
@@ -136,7 +143,7 @@ def tile_attend_lq_sgns_topk_kernel(tc, qT, k_words, k_scales, lq, offq, offs, o
         for b in range(B):
             quantize(1, b * NQ, (b + 1) * NQ)
 
-        k_scale = [k_scale0[:], k_scale1[:].bitcast(U8)]
+        k_scale = [plane[:].bitcast(U8) for plane in k_planes]
         scores = [psum.tile([P, P], F32, name=f"scores_{c}", tag=f"bank_{c}") for c in range(SLOTS // P)]
         for o in range(2):
             for c in range(SLOTS // P):

@@ -39,15 +39,15 @@ def tile_attend_lq_sgns_topk_kernel(tc, qT, k_words, k_scales, lq, offq, offs, o
         nc.sync.dma_start(slot_list[:], offs)
 
         scale_rows = k_scales.rearrange("o f t -> (o f) t").bitcast(I32)
-        nc.sync.dma_start(scale_pool[0:32, :], scale_rows)
+        nc.scalar.dma_start(scale_pool[0:32, :], scale_rows)
 
         lq_pool = keep.tile([P, T], F32, name="lq_pool")
-        nc.sync.dma_start(lq_pool[P - 1 : P, :], lq[0:1, :])
+        nc.scalar.dma_start(lq_pool[P - 1 : P, :], lq[0:1, :])
         nc.vector.memset(lq_pool[0 : P - 1, :], 0.0)
 
         k_planes = [keep.tile([P, SLOTS // 4], I32, name=f"k_plane_{o}", align_bytes=64) for o in range(2)]
         for o in range(2):
-            nc.vector.memset(k_planes[o][:], 0)
+            nc.gpsimd.memset(k_planes[o][:], 0)
 
         ident = keep.tile([P, P], F32, name="ident")
         make_identity(nc, ident[:])
@@ -169,7 +169,7 @@ def tile_attend_lq_sgns_topk_kernel(tc, qT, k_words, k_scales, lq, offq, offs, o
                 nc.vector.tensor_tensor(diff[:, cols], scores[c][:], lq_all[:, cols], ALU.subtract)
             nc.scalar.activation(grown[:, lo:hi], diff[:, lo:hi], ACT.Exp)
         nc.vector.tensor_scalar_min(capped[:], grown[:], EXP_CAP)
-        for lo, hi in ((0, 256), (256, 512), (512, 768), (768, 896), (896, 1024)):
+        for lo, hi in ((0, 128), (128, 320), (320, 512), (512, 768), (768, 1024)):
             cols = slice(lo, hi)
             nc.scalar.activation(logs[:, cols], capped[:, cols], ACT.Ln, bias=1.0)
             nc.vector.tensor_tensor(result[:, cols], logs[:, cols], diff[:, cols], ALU.max)

@@ -59,7 +59,7 @@ def tile_attend_lq_sgns_topk_kernel(tc, qT, k_words, k_scales, lq, offq, offs, o
             nc.sync.dma_start(raw[:], q_rows[o, :, r, :])
             return raw[:]
 
-        raw0 = [load_row(0, 0, "row_0"), load_row(0, 1, "first_then_cols")]
+        raw0 = [load_row(0, 0, "row_0"), load_row(0, 1, "row_1")]
         query_list = keep.tile([P, QUERIES // 16], U16, name="query_list")
         nc.sync.dma_start(query_list[:], offq)
         word_pool = keep.tile([P, T], I32, name="word_pool")
@@ -71,7 +71,7 @@ def tile_attend_lq_sgns_topk_kernel(tc, qT, k_words, k_scales, lq, offq, offs, o
             return [raw[:, 0, :], raw[:, 1, :]]
 
         raw0.append(load_row(0, 2, "row_2"))
-        raw0.append(load_row(0, 3, "row_then_lq"))
+        raw0.append(load_row(0, 3, "row_3"))
         raw1 = load_pair(1, 0, "row_4") + [load_row(1, r, f"row_{4 + r}") for r in range(2, 4)]
 
         scale_picked = keep.tile([P, SLOTS], U8, name="scale_picked", align_bytes=64)
@@ -91,18 +91,18 @@ def tile_attend_lq_sgns_topk_kernel(tc, qT, k_words, k_scales, lq, offq, offs, o
         word_halves = word_pairs[:].bitcast(U16).rearrange("p (n o) -> p o n", o=2)
         nc.vector.tensor_copy(k_codes[:], word_halves)
 
-        q_grouped = [keep.tile([P, QUERIES, 4], BF16, name=f"q_grouped_{o}", align_bytes=64) for o in range(2)]
+        q_grouped = [keep.tile([P, QUERIES, 4], BF16, name="q_grouped_0", align_bytes=64)]
         q_scales = [keep.tile([P, QUERIES], U8, name=f"q_scales_{o}", align_bytes=64) for o in range(2)]
 
         def scalar_row(r):
-            rounded = keep.tile([P, V], BF16, name=f"rounded_{r}")
+            rounded = keep.tile([P, V], BF16, name=f"rounded_{r}", tag=f"rounded_{r}", align_bytes=64)
             nc.scalar.activation(rounded[:], raw0[r], ACT.Copy)
             nc.scalar.activation(q_grouped[0][:, :, r], rounded[:].indirect(query_list[:]), ACT.Copy)
 
         scalar_row(0)
         scalar_row(1)
 
-        lq_cols = keep.tile([P, SLOTS // P], F32, name="lq_cols", tag="first_then_cols", align_bytes=64)
+        lq_cols = keep.tile([P, SLOTS // P], F32, name="lq_cols", tag="rounded_1", align_bytes=64)
         for b in range(B):
             turned = psum.tile([P, 4, P], F32, name=f"turned_{b}", tag=f"bank_{4 + b}")
             for j in range(4):
@@ -113,13 +113,20 @@ def tile_attend_lq_sgns_topk_kernel(tc, qT, k_words, k_scales, lq, offq, offs, o
         scalar_row(2)
         scalar_row(3)
 
-        lq_all = keep.tile([P, SLOTS], F32, name="lq_all", tag="row_then_lq", align_bytes=64)
+        q_grouped.append(keep.tile([P, QUERIES, 4], BF16, name="q_grouped_1", tag="row_3", align_bytes=64))
+        q_picked = keep.tile([P, 2, QUERIES], F32, name="q_picked", align_bytes=64)
+        for r in range(2):
+            nc.vector.tensor_copy(q_picked[:, r, :], raw1[r].indirect(query_list[:]))
+
+        lq_all = keep.tile([P, SLOTS], F32, name="lq_all", tag="rounded_3", align_bytes=64)
         for b in range(B):
             spread = psum.tile([P, N], F32, name=f"spread_{b}", tag=f"bank_{6 + b}")
             for j in range(4):
                 c = 4 * b + j
                 nc.tensor.transpose(spread[:, j * P : (j + 1) * P], lq_cols[:, c : c + 1].to_broadcast([P, P]), ident[:])
             nc.scalar.activation(lq_all[:, b * N : (b + 1) * N], spread[:], ACT.Copy)
+
+        nc.scalar.activation(q_grouped[1][:, :, 0:2], q_picked[:].rearrange("p r n -> p n r"), ACT.Copy)
 
         def gather_row(r, lo, hi):
             nc.vector.tensor_copy(q_grouped[1][:, lo:hi, r], raw1[r].indirect(query_list[:, lo // 16 : hi // 16]))
@@ -131,13 +138,12 @@ def tile_attend_lq_sgns_topk_kernel(tc, qT, k_words, k_scales, lq, offq, offs, o
                 q_grouped[o][:, lo:hi, :].rearrange("p n r -> p (n r)"),
             )
 
-        for r in range(3):
-            gather_row(r, 0, QUERIES)
         q_codes = [
-            keep.tile([P, QUERIES], U32, name="q_codes_0", tag="row_6", align_bytes=64),
+            keep.tile([P, QUERIES], U32, name="q_codes_0", tag="row_4", align_bytes=64),
             keep.tile([P, QUERIES], U32, name="q_codes_1", align_bytes=64),
         ]
         quantize(0, 0, QUERIES)
+        gather_row(2, 0, QUERIES)
         for b in range(B):
             gather_row(3, b * NQ, (b + 1) * NQ)
         for b in range(B):

@@ -169,14 +169,16 @@ def tile_attend_lq_sgns_topk_kernel(tc, qT, k_words, k_scales, lq, offq, offs, o
         capped = keep.tile([P, SLOTS], F32, name="capped")
         logs = keep.tile([P, SLOTS], F32, name="logs")
         result = keep.tile([P, SLOTS], F32, name="result")
-        for lo, hi in ((0, 128), (128, 384), (384, 640), (640, 896), (896, 1024)):
+        for lo, hi in [(c * P, (c + 1) * P) for c in range(SLOTS // P)]:
             for c in range(lo // P, hi // P):
                 cols = slice(c * P, (c + 1) * P)
                 nc.vector.tensor_tensor(diff[:, cols], scores[c][:], lq_all[:, cols], ALU.subtract)
             nc.scalar.activation(grown[:, lo:hi], diff[:, lo:hi], ACT.Exp)
         nc.vector.tensor_scalar_min(capped[:], grown[:], EXP_CAP)
         for lo, hi in ((0, 128), (128, 320), (320, 512), (512, 768), (768, 1024)):
-            cols = slice(lo, hi)
-            nc.scalar.activation(logs[:, cols], capped[:, cols], ACT.Ln, bias=1.0)
-            nc.vector.tensor_tensor(result[:, cols], logs[:, cols], diff[:, cols], ALU.max)
-            nc.sync.dma_start(out[lo // N, :, lo % N : lo % N + hi - lo], result[:, cols])
+            piece = hi - lo if hi - lo <= P else (hi - lo) // 2
+            for start in range(lo, hi, piece):
+                cols = slice(start, start + piece)
+                nc.scalar.activation(logs[:, cols], capped[:, cols], ACT.Ln, bias=1.0)
+                nc.vector.tensor_tensor(result[:, cols], logs[:, cols], diff[:, cols], ALU.max)
+            nc.sync.dma_start(out[lo // N, :, lo % N : lo % N + hi - lo], result[:, lo:hi])

@@ -1,3 +1,4 @@
+import math
 from contextlib import ExitStack
 
 import concourse.mybir as mybir
@@ -20,7 +21,8 @@ SLOTS = B * N
 QUERIES = B * NQ
 HALF = V // 2
 CHUNK = 256
-EXP_CAP = float(2**43)
+KNEE = 20.0
+SHRINK = math.exp(KNEE) / KNEE
 FLOPS = 2 * B * NQ * N * D
 BYTES = 4 * D * V + P * T * 4 + 2 * 16 * T + 4 * T + 2 * P * (16 + 64) + 4 * B * NQ * N
 
@@ -31,7 +33,7 @@ def tile_attend_lq_sgns_topk_kernel(tc, qT, k_words, k_scales, lq, offq, offs, o
         keep = ctx.enter_context(tc.tile_pool(name="keep", bufs=1))
         psum = ctx.enter_context(tc.psum_pool(name="psum", bufs=1))
 
-        scale_pool = keep.tile([P, T // 4], I32, name="scale_pool")
+        scale_pool = keep.tile([P, T // 4], I32, name="scale_pool", tag="scales", align_bytes=64)
         nc.gpsimd.memset(scale_pool[32:64, :], 0)
         nc.gpsimd.memset(scale_pool[64:128, :], 0)
 
@@ -44,10 +46,6 @@ def tile_attend_lq_sgns_topk_kernel(tc, qT, k_words, k_scales, lq, offq, offs, o
         lq_pool = keep.tile([P, T], F32, name="lq_pool")
         nc.scalar.dma_start(lq_pool[P - 1 : P, :], lq[0:1, :])
         nc.vector.memset(lq_pool[0 : P - 1, :], 0.0)
-
-        k_planes = [keep.tile([P, SLOTS // 4], I32, name=f"k_plane_{o}", align_bytes=64) for o in range(2)]
-        for o in range(2):
-            nc.gpsimd.memset(k_planes[o][:], 0)
 
         ident = keep.tile([P, P], F32, name="ident")
         make_identity(nc, ident[:])
@@ -76,6 +74,8 @@ def tile_attend_lq_sgns_topk_kernel(tc, qT, k_words, k_scales, lq, offq, offs, o
 
         scale_picked = keep.tile([P, SLOTS], U8, name="scale_picked", align_bytes=64)
         nc.vector.tensor_copy(scale_picked[:], scale_pool[:].bitcast(U8).indirect(slot_list[:]))
+        planes = keep.tile([P, T // 4], I32, name="planes", tag="scales", align_bytes=64)
+        k_planes = [planes[:, o * (SLOTS // 4) : (o + 1) * (SLOTS // 4)] for o in range(2)]
         for o, queue in enumerate((nc.gpsimd, nc.sync)):
             for quad in range(4):
                 row = 16 * o + 4 * quad
@@ -103,12 +103,14 @@ def tile_attend_lq_sgns_topk_kernel(tc, qT, k_words, k_scales, lq, offq, offs, o
         scalar_row(1)
 
         lq_cols = keep.tile([P, SLOTS // P], F32, name="lq_cols", tag="rounded_1", align_bytes=64)
+        exp_bias = keep.tile([P, SLOTS // P], F32, name="exp_bias")
         for b in range(B):
             turned = psum.tile([P, 4, P], F32, name=f"turned_{b}", tag=f"bank_{4 + b}")
             for j in range(4):
                 c = 4 * b + j
                 nc.tensor.transpose(turned[:, j, :], lq_row[:, c * P : (c + 1) * P], ident[:])
-            nc.scalar.activation(lq_cols[:, 4 * b : 4 * b + 4], turned[:, :, P - 1], ACT.Copy)
+            nc.scalar.activation(lq_cols[:, 4 * b : 4 * b + 4], turned[:, :, P - 1], ACT.Copy, scale=-1.0)
+            nc.scalar.activation(exp_bias[:, 4 * b : 4 * b + 4], turned[:, :, P - 1], ACT.Copy, scale=-1.0, bias=-math.log(SHRINK))
 
         scalar_row(2)
         scalar_row(3)
@@ -117,14 +119,6 @@ def tile_attend_lq_sgns_topk_kernel(tc, qT, k_words, k_scales, lq, offq, offs, o
         q_picked = keep.tile([P, 2, QUERIES], F32, name="q_picked", align_bytes=64)
         for r in range(2):
             nc.vector.tensor_copy(q_picked[:, r, :], raw1[r].indirect(query_list[:]))
-
-        lq_all = keep.tile([P, SLOTS], F32, name="lq_all", tag="rounded_3", align_bytes=64)
-        for b in range(B):
-            spread = psum.tile([P, N], F32, name=f"spread_{b}", tag=f"bank_{6 + b}")
-            for j in range(4):
-                c = 4 * b + j
-                nc.tensor.transpose(spread[:, j * P : (j + 1) * P], lq_cols[:, c : c + 1].to_broadcast([P, P]), ident[:])
-            nc.scalar.activation(lq_all[:, b * N : (b + 1) * N], spread[:], ACT.Copy)
 
         nc.scalar.activation(q_grouped[1][:, :, 0:2], q_picked[:].rearrange("p r n -> p n r"), ACT.Copy)
 
@@ -149,36 +143,38 @@ def tile_attend_lq_sgns_topk_kernel(tc, qT, k_words, k_scales, lq, offq, offs, o
         for b in range(B):
             quantize(1, b * NQ, (b + 1) * NQ)
 
-        k_scale = [plane[:].bitcast(U8) for plane in k_planes]
+        k_scale = [plane.bitcast(U8) for plane in k_planes]
         scores = [psum.tile([P, P], F32, name=f"scores_{c}", tag=f"bank_{c}") for c in range(SLOTS // P)]
         for o in range(2):
             for c in range(SLOTS // P):
                 b = c * P // N
                 nc.tensor.matmul_mx(
                     scores[c][:],
-                    lhsT=q_codes[o][:, b * NQ : (b + 1) * NQ].bitcast(FP8X4),
-                    lhsT_scale=q_scales[o][:, b * NQ : (b + 1) * NQ],
-                    rhs=k_codes[:, o, c * P : (c + 1) * P].bitcast(FP4X4),
-                    rhs_scale=k_scale[o][:, c * P : (c + 1) * P],
+                    lhsT=k_codes[:, o, c * P : (c + 1) * P].bitcast(FP4X4),
+                    lhsT_scale=k_scale[o][:, c * P : (c + 1) * P],
+                    rhs=q_codes[o][:, b * NQ : (b + 1) * NQ].bitcast(FP8X4),
+                    rhs_scale=q_scales[o][:, b * NQ : (b + 1) * NQ],
                     start=(o == 0),
                     stop=(o == 1),
                 )
 
-        diff = keep.tile([P, SLOTS], F32, name="diff")
+        floor = keep.tile([P, SLOTS], F32, name="floor")
         grown = keep.tile([P, SLOTS], F32, name="grown")
-        capped = keep.tile([P, SLOTS], F32, name="capped")
+        folded = keep.tile([P, SLOTS], F32, name="folded")
         logs = keep.tile([P, SLOTS], F32, name="logs")
         result = keep.tile([P, SLOTS], F32, name="result")
-        for lo, hi in [(c * P, (c + 1) * P) for c in range(SLOTS // P)]:
-            for c in range(lo // P, hi // P):
+        backs = []
+        for c in range(SLOTS // P):
+            cols = slice(c * P, (c + 1) * P)
+            nc.scalar.activation(grown[:, cols], scores[c][:], ACT.Exp, bias=exp_bias[:, c : c + 1])
+            nc.vector.tensor_scalar(floor[:, cols], scores[c][:], lq_cols[:, c : c + 1], KNEE, ALU.add, ALU.max)
+            nc.vector.tensor_tensor(folded[:, cols], grown[:, cols], floor[:, cols], ALU.min)
+            backs.append(psum.tile([P, P], F32, name=f"back_{c}", tag=f"bank_{c}"))
+            nc.tensor.transpose(backs[c][:], folded[:, cols], ident[:])
+        for first, last in ((0, 1), (1, 2), (2, 4), (4, 6), (6, 8)):
+            for c in range(first, last):
                 cols = slice(c * P, (c + 1) * P)
-                nc.vector.tensor_tensor(diff[:, cols], scores[c][:], lq_all[:, cols], ALU.subtract)
-            nc.scalar.activation(grown[:, lo:hi], diff[:, lo:hi], ACT.Exp)
-        nc.vector.tensor_scalar_min(capped[:], grown[:], EXP_CAP)
-        for lo, hi in ((0, 128), (128, 320), (320, 512), (512, 768), (768, 1024)):
-            piece = hi - lo if hi - lo <= P else (hi - lo) // 2
-            for start in range(lo, hi, piece):
-                cols = slice(start, start + piece)
-                nc.scalar.activation(logs[:, cols], capped[:, cols], ACT.Ln, bias=1.0)
-                nc.vector.tensor_tensor(result[:, cols], logs[:, cols], diff[:, cols], ALU.max)
+                nc.scalar.activation(logs[:, cols], backs[c][:], ACT.Ln, bias=1.0, scale=SHRINK)
+                nc.vector.tensor_tensor(result[:, cols], logs[:, cols], backs[c][:], ALU.max)
+            lo, hi = first * P, last * P
             nc.sync.dma_start(out[lo // N, :, lo % N : lo % N + hi - lo], result[:, lo:hi])

@@ -33,7 +33,7 @@ def tile_attend_lq_sgns_topk_kernel(tc, qT, k_words, k_scales, lq, offq, offs, o
         keep = ctx.enter_context(tc.tile_pool(name="keep", bufs=1))
         psum = ctx.enter_context(tc.psum_pool(name="psum", bufs=1))
 
-        scale_pool = keep.tile([P, T // 4], I32, name="scale_pool", tag="scales", align_bytes=64)
+        scale_pool = keep.tile([P, T // 4], I32, name="scale_pool")
         nc.gpsimd.memset(scale_pool[32:64, :], 0)
         nc.gpsimd.memset(scale_pool[64:128, :], 0)
 
@@ -74,8 +74,7 @@ def tile_attend_lq_sgns_topk_kernel(tc, qT, k_words, k_scales, lq, offq, offs, o
 
         scale_picked = keep.tile([P, SLOTS], U8, name="scale_picked", align_bytes=64)
         nc.vector.tensor_copy(scale_picked[:], scale_pool[:].bitcast(U8).indirect(slot_list[:]))
-        planes = keep.tile([P, T // 4], I32, name="planes", tag="scales", align_bytes=64)
-        k_planes = [planes[:, o * (SLOTS // 4) : (o + 1) * (SLOTS // 4)] for o in range(2)]
+        k_planes = [keep.tile([P, SLOTS // 4], I32, name=f"k_plane_{o}", align_bytes=64) for o in range(2)]
         for o, queue in enumerate((nc.gpsimd, nc.sync)):
             for quad in range(4):
                 row = 16 * o + 4 * quad
@@ -99,21 +98,18 @@ def tile_attend_lq_sgns_topk_kernel(tc, qT, k_words, k_scales, lq, offq, offs, o
             nc.scalar.activation(rounded[:], raw0[r], ACT.Copy)
             nc.scalar.activation(q_grouped[0][:, :, r], rounded[:].indirect(query_list[:]), ACT.Copy)
 
-        scalar_row(0)
-        scalar_row(1)
+        for r in range(4):
+            scalar_row(r)
 
-        lq_cols = keep.tile([P, SLOTS // P], F32, name="lq_cols", tag="rounded_1", align_bytes=64)
+        lq_cols = keep.tile([P, SLOTS // P], F32, name="lq_cols", tag="rounded_3", align_bytes=64)
         exp_bias = keep.tile([P, SLOTS // P], F32, name="exp_bias")
         for b in range(B):
-            turned = psum.tile([P, 4, P], F32, name=f"turned_{b}", tag=f"bank_{4 + b}")
+            turned = psum.tile([P, 4, P], F32, name=f"turned_{b}", tag=f"bank_{6 + b}")
             for j in range(4):
                 c = 4 * b + j
                 nc.tensor.transpose(turned[:, j, :], lq_row[:, c * P : (c + 1) * P], ident[:])
             nc.scalar.activation(lq_cols[:, 4 * b : 4 * b + 4], turned[:, :, P - 1], ACT.Copy, scale=-1.0)
-            nc.scalar.activation(exp_bias[:, 4 * b : 4 * b + 4], turned[:, :, P - 1], ACT.Copy, scale=-1.0, bias=-math.log(SHRINK))
-
-        scalar_row(2)
-        scalar_row(3)
+        nc.scalar.activation(exp_bias[:], lq_cols[:], ACT.Copy, bias=-math.log(SHRINK))
 
         q_grouped.append(keep.tile([P, QUERIES, 4], BF16, name="q_grouped_1", tag="row_3", align_bytes=64))
         q_picked = keep.tile([P, 2, QUERIES], F32, name="q_picked", align_bytes=64)
@@ -143,7 +139,7 @@ def tile_attend_lq_sgns_topk_kernel(tc, qT, k_words, k_scales, lq, offq, offs, o
         for b in range(B):
             quantize(1, b * NQ, (b + 1) * NQ)
 
-        k_scale = [plane.bitcast(U8) for plane in k_planes]
+        k_scale = [plane[:].bitcast(U8) for plane in k_planes]
         scores = [psum.tile([P, P], F32, name=f"scores_{c}", tag=f"bank_{c}") for c in range(SLOTS // P)]
         for o in range(2):
             for c in range(SLOTS // P):
@@ -168,9 +164,11 @@ def tile_attend_lq_sgns_topk_kernel(tc, qT, k_words, k_scales, lq, offq, offs, o
             cols = slice(c * P, (c + 1) * P)
             nc.scalar.activation(grown[:, cols], scores[c][:], ACT.Exp, bias=exp_bias[:, c : c + 1])
             nc.vector.tensor_scalar(floor[:, cols], scores[c][:], lq_cols[:, c : c + 1], KNEE, ALU.add, ALU.max)
-            nc.vector.tensor_tensor(folded[:, cols], grown[:, cols], floor[:, cols], ALU.min)
+        for lo in range(0, SLOTS, CHUNK):
+            nc.vector.tensor_tensor(folded[:, lo : lo + CHUNK], grown[:, lo : lo + CHUNK], floor[:, lo : lo + CHUNK], ALU.min)
+        for c in range(SLOTS // P):
             backs.append(psum.tile([P, P], F32, name=f"back_{c}", tag=f"bank_{c}"))
-            nc.tensor.transpose(backs[c][:], folded[:, cols], ident[:])
+            nc.tensor.transpose(backs[c][:], folded[:, c * P : (c + 1) * P], ident[:])
         for first, last in ((0, 1), (1, 2), (2, 4), (4, 6), (6, 8)):
             for c in range(first, last):
                 cols = slice(c * P, (c + 1) * P)

@@ -34,8 +34,8 @@ def tile_attend_lq_sgns_topk_kernel(tc, qT, k_words, k_scales, lq, offq, offs, o
         psum = ctx.enter_context(tc.psum_pool(name="psum", bufs=1))
 
         scale_pool = keep.tile([P, T // 4], I32, name="scale_pool")
-        nc.gpsimd.memset(scale_pool[32:64, :], 0)
-        nc.gpsimd.memset(scale_pool[64:128, :], 0)
+        nc.vector.memset(scale_pool[32:64, :], 0)
+        nc.vector.memset(scale_pool[64:128, :], 0)
 
         slot_list = keep.tile([P, SLOTS // 16], U16, name="slot_list")
         nc.sync.dma_start(slot_list[:], offs)
@@ -48,7 +48,8 @@ def tile_attend_lq_sgns_topk_kernel(tc, qT, k_words, k_scales, lq, offq, offs, o
         nc.vector.memset(lq_pool[0 : P - 1, :], 0.0)
 
         ident = keep.tile([P, P], F32, name="ident")
-        make_identity(nc, ident[:])
+        nc.vector.memset(ident[:], 0.0)
+        make_identity(nc, ident[:], nomemset=True)
 
         q_rows = qT.rearrange("(o p r) n -> o p r n", o=2, r=4)
 
@@ -57,20 +58,20 @@ def tile_attend_lq_sgns_topk_kernel(tc, qT, k_words, k_scales, lq, offq, offs, o
             nc.sync.dma_start(raw[:], q_rows[o, :, r, :])
             return raw[:]
 
-        raw0 = [load_row(0, 0, "row_0"), load_row(0, 1, "row_1")]
-        query_list = keep.tile([P, QUERIES // 16], U16, name="query_list")
-        nc.sync.dma_start(query_list[:], offq)
-        word_pool = keep.tile([P, T], I32, name="word_pool")
-        nc.sync.dma_start(word_pool[:], k_words[0].rearrange("p t b -> p (t b)").bitcast(I32))
-
         def load_pair(o, r, tag):
             raw = keep.tile([P, 2, V], F32, name=f"raw_{o}_{r}", tag=tag, align_bytes=64)
             nc.sync.dma_start(raw[:], q_rows[o, :, r : r + 2, :])
             return [raw[:, 0, :], raw[:, 1, :]]
 
+        raw0 = load_pair(0, 0, "row_0")
+        query_list = keep.tile([P, QUERIES // 16], U16, name="query_list")
+        nc.sync.dma_start(query_list[:], offq)
+        word_pool = keep.tile([P, T], I32, name="word_pool")
+        nc.sync.dma_start(word_pool[:], k_words[0].rearrange("p t b -> p (t b)").bitcast(I32))
+
         raw0.append(load_row(0, 2, "row_2"))
         raw0.append(load_row(0, 3, "row_3"))
-        raw1 = load_pair(1, 0, "row_4") + [load_row(1, r, f"row_{4 + r}") for r in range(2, 4)]
+        raw1 = [load_row(1, r, f"row_{4 + r}") for r in range(4)]
 
         scale_picked = keep.tile([P, SLOTS], U8, name="scale_picked", align_bytes=64)
         nc.vector.tensor_copy(scale_picked[:], scale_pool[:].bitcast(U8).indirect(slot_list[:]))
@@ -129,7 +130,7 @@ def tile_attend_lq_sgns_topk_kernel(tc, qT, k_words, k_scales, lq, offq, offs, o
             )
 
         q_codes = [
-            keep.tile([P, QUERIES], U32, name="q_codes_0", tag="row_4", align_bytes=64),
+            keep.tile([P, QUERIES], U32, name="q_codes_0", tag="row_5", align_bytes=64),
             keep.tile([P, QUERIES], U32, name="q_codes_1", align_bytes=64),
         ]
         quantize(0, 0, QUERIES)

@@ -58,12 +58,7 @@ def tile_attend_lq_sgns_topk_kernel(tc, qT, k_words, k_scales, lq, offq, offs, o
             nc.sync.dma_start(raw[:], q_rows[o, :, r, :])
             return raw[:]
 
-        def load_pair(o, r, tag):
-            raw = keep.tile([P, 2, V], F32, name=f"raw_{o}_{r}", tag=tag, align_bytes=64)
-            nc.sync.dma_start(raw[:], q_rows[o, :, r : r + 2, :])
-            return [raw[:, 0, :], raw[:, 1, :]]
-
-        raw0 = load_pair(0, 0, "row_0")
+        raw0 = [load_row(0, 0, "row_0"), load_row(0, 1, "row_1")]
         query_list = keep.tile([P, QUERIES // 16], U16, name="query_list")
         nc.sync.dma_start(query_list[:], offq)
         word_pool = keep.tile([P, T], I32, name="word_pool")
@@ -94,15 +89,14 @@ def tile_attend_lq_sgns_topk_kernel(tc, qT, k_words, k_scales, lq, offq, offs, o
         q_grouped = [keep.tile([P, QUERIES, 4], BF16, name="q_grouped_0", align_bytes=64)]
         q_scales = [keep.tile([P, QUERIES], U8, name=f"q_scales_{o}", align_bytes=64) for o in range(2)]
 
-        def scalar_row(r):
-            rounded = keep.tile([P, V], BF16, name=f"rounded_{r}", tag=f"rounded_{r}", align_bytes=64)
-            nc.scalar.activation(rounded[:], raw0[r], ACT.Copy)
-            nc.scalar.activation(q_grouped[0][:, :, r], rounded[:].indirect(query_list[:]), ACT.Copy)
+        rounded = [keep.tile([P, V], BF16, name=f"rounded_{r}", align_bytes=64) for r in range(4)]
+        for pair in ((0, 1), (2, 3)):
+            for r in pair:
+                nc.scalar.activation(rounded[r][:], raw0[r], ACT.Copy)
+            for r in pair:
+                nc.scalar.activation(q_grouped[0][:, :, r], rounded[r][:].indirect(query_list[:]), ACT.Copy)
 
-        for r in range(4):
-            scalar_row(r)
-
-        lq_cols = keep.tile([P, SLOTS // P], F32, name="lq_cols", tag="rounded_3", align_bytes=64)
+        lq_cols = keep.tile([P, SLOTS // P], F32, name="lq_cols", tag="row_3", align_bytes=64)
         exp_bias = keep.tile([P, SLOTS // P], F32, name="exp_bias")
         for b in range(B):
             turned = psum.tile([P, 4, P], F32, name=f"turned_{b}", tag=f"bank_{6 + b}")
@@ -112,7 +106,7 @@ def tile_attend_lq_sgns_topk_kernel(tc, qT, k_words, k_scales, lq, offq, offs, o
             nc.scalar.activation(lq_cols[:, 4 * b : 4 * b + 4], turned[:, :, P - 1], ACT.Copy, scale=-1.0)
         nc.scalar.activation(exp_bias[:], lq_cols[:], ACT.Copy, bias=-math.log(SHRINK))
 
-        q_grouped.append(keep.tile([P, QUERIES, 4], BF16, name="q_grouped_1", tag="row_3", align_bytes=64))
+        q_grouped.append(keep.tile([P, QUERIES, 4], BF16, name="q_grouped_1", align_bytes=64))
         q_picked = keep.tile([P, 2, QUERIES], F32, name="q_picked", align_bytes=64)
         for r in range(2):
             nc.vector.tensor_copy(q_picked[:, r, :], raw1[r].indirect(query_list[:]))

@@ -22,7 +22,8 @@ QUERIES = B * NQ
 HALF = V // 2
 CHUNK = 256
 KNEE = 20.0
-SHRINK = math.exp(KNEE) / KNEE
+LIFT = 40.0
+SHRINK = math.exp(KNEE) / (KNEE + LIFT)
 FLOPS = 2 * B * NQ * N * D
 BYTES = 4 * D * V + P * T * 4 + 2 * 16 * T + 4 * T + 2 * P * (16 + 64) + 4 * B * NQ * N
 
@@ -58,7 +59,9 @@ def tile_attend_lq_sgns_topk_kernel(tc, qT, k_words, k_scales, lq, offq, offs, o
             nc.sync.dma_start(raw[:], q_rows[o, :, r, :])
             return raw[:]
 
-        raw0 = [load_row(0, 0, "row_0"), load_row(0, 1, "row_1")]
+        first_pair = keep.tile([P, 2, V], F32, name="first_pair")
+        nc.sync.dma_start(first_pair[:], q_rows[0, :, 0:2, :])
+        raw0 = [first_pair[:, 0, :], first_pair[:, 1, :]]
         query_list = keep.tile([P, QUERIES // 16], U16, name="query_list")
         nc.sync.dma_start(query_list[:], offq)
         word_pool = keep.tile([P, T], I32, name="word_pool")
@@ -96,22 +99,22 @@ def tile_attend_lq_sgns_topk_kernel(tc, qT, k_words, k_scales, lq, offq, offs, o
             for r in pair:
                 nc.scalar.activation(q_grouped[0][:, :, r], rounded[r][:].indirect(query_list[:]), ACT.Copy)
 
-        lq_cols = keep.tile([P, SLOTS // P], F32, name="lq_cols", tag="row_3", align_bytes=64)
-        exp_bias = keep.tile([P, SLOTS // P], F32, name="exp_bias")
-        for b in range(B):
-            turned = psum.tile([P, 4, P], F32, name=f"turned_{b}", tag=f"bank_{6 + b}")
-            for j in range(4):
-                c = 4 * b + j
-                nc.tensor.transpose(turned[:, j, :], lq_row[:, c * P : (c + 1) * P], ident[:])
-            nc.scalar.activation(lq_cols[:, 4 * b : 4 * b + 4], turned[:, :, P - 1], ACT.Copy, scale=-1.0)
-        nc.scalar.activation(exp_bias[:], lq_cols[:], ACT.Copy, bias=-math.log(SHRINK))
-
         q_grouped.append(keep.tile([P, QUERIES, 4], BF16, name="q_grouped_1", align_bytes=64))
         q_picked = keep.tile([P, 2, QUERIES], F32, name="q_picked", align_bytes=64)
         for r in range(2):
             nc.vector.tensor_copy(q_picked[:, r, :], raw1[r].indirect(query_list[:]))
 
         nc.scalar.activation(q_grouped[1][:, :, 0:2], q_picked[:].rearrange("p r n -> p n r"), ACT.Copy)
+
+        exp_bias = keep.tile([P, SLOTS // P], F32, name="exp_bias", tag="row_3", align_bytes=64)
+        lift_bias = keep.tile([P, SLOTS // P], F32, name="lift_bias")
+        for b in range(B):
+            turned = psum.tile([P, 4, P], F32, name=f"turned_{b}", tag=f"bank_{6 + b}")
+            for j in range(4):
+                c = 4 * b + j
+                nc.tensor.transpose(turned[:, j, :], lq_row[:, c * P : (c + 1) * P], ident[:])
+            nc.scalar.activation(exp_bias[:, 4 * b : 4 * b + 4], turned[:, :, P - 1], ACT.Copy, scale=-1.0, bias=-math.log(SHRINK))
+        nc.scalar.activation(lift_bias[:], exp_bias[:], ACT.Copy, bias=math.log(SHRINK) + LIFT)
 
         def gather_row(r, lo, hi):
             nc.vector.tensor_copy(q_grouped[1][:, lo:hi, r], raw1[r].indirect(query_list[:, lo // 16 : hi // 16]))
@@ -149,7 +152,7 @@ def tile_attend_lq_sgns_topk_kernel(tc, qT, k_words, k_scales, lq, offq, offs, o
                     stop=(o == 1),
                 )
 
-        floor = keep.tile([P, SLOTS], F32, name="floor")
+        lesser = keep.tile([P, SLOTS], F32, name="lesser")
         grown = keep.tile([P, SLOTS], F32, name="grown")
         folded = keep.tile([P, SLOTS], F32, name="folded")
         logs = keep.tile([P, SLOTS], F32, name="logs")
@@ -158,9 +161,9 @@ def tile_attend_lq_sgns_topk_kernel(tc, qT, k_words, k_scales, lq, offq, offs, o
         for c in range(SLOTS // P):
             cols = slice(c * P, (c + 1) * P)
             nc.scalar.activation(grown[:, cols], scores[c][:], ACT.Exp, bias=exp_bias[:, c : c + 1])
-            nc.vector.tensor_scalar(floor[:, cols], scores[c][:], lq_cols[:, c : c + 1], KNEE, ALU.add, ALU.max)
+            nc.vector.scalar_tensor_tensor(lesser[:, cols], scores[c][:], lift_bias[:, c : c + 1], grown[:, cols], ALU.add, ALU.min)
         for lo in range(0, SLOTS, CHUNK):
-            nc.vector.tensor_tensor(folded[:, lo : lo + CHUNK], grown[:, lo : lo + CHUNK], floor[:, lo : lo + CHUNK], ALU.min)
+            nc.vector.tensor_scalar_max(folded[:, lo : lo + CHUNK], lesser[:, lo : lo + CHUNK], 0.0)
         for c in range(SLOTS // P):
             backs.append(psum.tile([P, P], F32, name=f"back_{c}", tag=f"bank_{c}"))
             nc.tensor.transpose(backs[c][:], folded[:, c * P : (c + 1) * P], ident[:])
@@ -168,6 +171,6 @@ def tile_attend_lq_sgns_topk_kernel(tc, qT, k_words, k_scales, lq, offq, offs, o
             for c in range(first, last):
                 cols = slice(c * P, (c + 1) * P)
                 nc.scalar.activation(logs[:, cols], backs[c][:], ACT.Ln, bias=1.0, scale=SHRINK)
-                nc.vector.tensor_tensor(result[:, cols], logs[:, cols], backs[c][:], ALU.max)
+                nc.vector.scalar_tensor_tensor(result[:, cols], backs[c][:], -LIFT, logs[:, cols], ALU.add, ALU.max)
             lo, hi = first * P, last * P
             nc.sync.dma_start(out[lo // N, :, lo % N : lo % N + hi - lo], result[:, lo:hi])

@@ -34,79 +34,79 @@ def tile_attend_lq_sgns_topk_kernel(tc, qT, k_words, k_scales, lq, offq, offs, o
         keep = ctx.enter_context(tc.tile_pool(name="keep", bufs=1))
         psum = ctx.enter_context(tc.psum_pool(name="psum", bufs=1))
 
-        scale_pool = keep.tile([P, T // 4], I32, name="scale_pool")
-        nc.vector.memset(scale_pool[32:64, :], 0)
-        nc.vector.memset(scale_pool[64:128, :], 0)
-
         slot_list = keep.tile([P, SLOTS // 16], U16, name="slot_list")
         nc.sync.dma_start(slot_list[:], offs)
 
+        scale_pool = keep.tile([P, T // 4], I32, name="scale_pool", tag="scale_pool", align_bytes=64)
+        nc.vector.memset(scale_pool[32:64, :], 0)
+        nc.vector.memset(scale_pool[64:128, :], 0)
         scale_rows = k_scales.rearrange("o f t -> (o f) t").bitcast(I32)
         nc.scalar.dma_start(scale_pool[0:32, :], scale_rows)
 
         lq_pool = keep.tile([P, T], F32, name="lq_pool")
         nc.scalar.dma_start(lq_pool[P - 1 : P, :], lq[0:1, :])
-        nc.vector.memset(lq_pool[0 : P - 1, :], 0.0)
+        nc.gpsimd.memset(lq_pool[0 : P - 1, :], 0.0)
+
+        word_pool = keep.tile([P, T], I32, name="word_pool", tag="word_pool", align_bytes=64)
+        nc.sync.dma_start(word_pool[:], k_words[0].rearrange("p t b -> p (t b)").bitcast(I32))
+
+        query_list = keep.tile([P, QUERIES // 16], U16, name="query_list")
+        nc.sync.dma_start(query_list[:], offq)
 
         ident = keep.tile([P, P], F32, name="ident")
-        nc.vector.memset(ident[:], 0.0)
-        make_identity(nc, ident[:], nomemset=True)
+        make_identity(nc, ident[:])
 
         q_rows = qT.rearrange("(o p r) n -> o p r n", o=2, r=4)
 
-        def load_row(o, r, tag):
-            raw = keep.tile([P, V], F32, name=f"raw_{o}_{r}", tag=tag, align_bytes=64)
-            nc.sync.dma_start(raw[:], q_rows[o, :, r, :])
-            return raw[:]
+        def load_rows(o, lo, hi, tag):
+            raw = keep.tile([P, hi - lo, V], F32, name=f"raw_{o}_{lo}", tag=tag, align_bytes=64)
+            nc.sync.dma_start(raw[:], q_rows[o, :, lo:hi, :])
+            return [raw[:, r, :] for r in range(hi - lo)]
 
-        first_pair = keep.tile([P, 2, V], F32, name="first_pair")
-        nc.sync.dma_start(first_pair[:], q_rows[0, :, 0:2, :])
-        raw0 = [first_pair[:, 0, :], first_pair[:, 1, :]]
-        query_list = keep.tile([P, QUERIES // 16], U16, name="query_list")
-        nc.sync.dma_start(query_list[:], offq)
-        word_pool = keep.tile([P, T], I32, name="word_pool")
-        nc.sync.dma_start(word_pool[:], k_words[0].rearrange("p t b -> p (t b)").bitcast(I32))
-
-        raw0.append(load_row(0, 2, "row_2"))
-        raw0.append(load_row(0, 3, "row_3"))
-        raw1 = [load_row(1, r, f"row_{4 + r}") for r in range(4)]
+        raw0 = load_rows(0, 0, 2, "first_rows") + load_rows(0, 2, 4, "second_rows")
 
         scale_picked = keep.tile([P, SLOTS], U8, name="scale_picked", align_bytes=64)
         nc.vector.tensor_copy(scale_picked[:], scale_pool[:].bitcast(U8).indirect(slot_list[:]))
-        k_planes = [keep.tile([P, SLOTS // 4], I32, name=f"k_plane_{o}", align_bytes=64) for o in range(2)]
-        for o, queue in enumerate((nc.gpsimd, nc.sync)):
-            for quad in range(4):
+        k_planes = []
+
+        def lay_plane(o, tag):
+            k_planes.append(keep.tile([P, SLOTS // 4], I32, name=f"k_plane_{o}", tag=tag, align_bytes=64))
+            for quad in (0, 2, 1, 3):
                 row = 16 * o + 4 * quad
-                queue.dma_start(k_planes[o][32 * quad : 32 * quad + 4, :], scale_picked[row : row + 4, :].bitcast(I32))
+                nc.sync.dma_start(k_planes[o][32 * quad : 32 * quad + 4, :], scale_picked[row : row + 4, :].bitcast(I32))
+
+        lay_plane(0, "first_plane")
+        raw1 = load_rows(1, 0, 2, "scale_pool")
 
         lq_row = keep.tile([P, SLOTS], F32, name="lq_row")
-        nc.vector.tensor_copy(lq_row[:], lq_pool[:].indirect(slot_list[:]))
+        nc.scalar.activation(lq_row[:, 0:N], lq_pool[:].indirect(slot_list[:, 0 : N // 16]), ACT.Copy)
 
         word_pairs = keep.tile([P, SLOTS], U32, name="word_pairs")
         nc.vector.tensor_copy(word_pairs[:], word_pool[:].bitcast(U32).indirect(slot_list[:]))
 
+        raw1 = raw1 + load_rows(1, 2, 3, "word_pool")
+
         k_codes = keep.tile([P, 2, SLOTS], U16, name="k_codes", align_bytes=64)
         word_halves = word_pairs[:].bitcast(U16).rearrange("p (n o) -> p o n", o=2)
         nc.vector.tensor_copy(k_codes[:], word_halves)
+        nc.vector.tensor_copy(lq_row[:, N:SLOTS], lq_pool[:].indirect(slot_list[:, N // 16 : SLOTS // 16]))
 
-        q_grouped = [keep.tile([P, QUERIES, 4], BF16, name="q_grouped_0", align_bytes=64)]
+        q_grouped = [keep.tile([P, QUERIES, 4], BF16, name=f"q_grouped_{o}", align_bytes=64) for o in range(2)]
         q_scales = [keep.tile([P, QUERIES], U8, name=f"q_scales_{o}", align_bytes=64) for o in range(2)]
 
-        rounded = [keep.tile([P, V], BF16, name=f"rounded_{r}", align_bytes=64) for r in range(4)]
-        for pair in ((0, 1), (2, 3)):
-            for r in pair:
-                nc.scalar.activation(rounded[r][:], raw0[r], ACT.Copy)
-            for r in pair:
-                nc.scalar.activation(q_grouped[0][:, :, r], rounded[r][:].indirect(query_list[:]), ACT.Copy)
+        picked0 = keep.tile([P, 4, QUERIES], F32, name="picked0", align_bytes=64)
+        for r in range(4):
+            nc.scalar.activation(picked0[:, r, :], raw0[r].indirect(query_list[:]), ACT.Copy)
+        raw1 = raw1 + load_rows(1, 3, 4, "first_rows")
+        lay_plane(1, "second_rows")
+        nc.vector.tensor_copy(q_grouped[0][:], picked0[:].rearrange("p r n -> p n r"))
 
-        q_grouped.append(keep.tile([P, QUERIES, 4], BF16, name="q_grouped_1", align_bytes=64))
         q_picked = keep.tile([P, 2, QUERIES], F32, name="q_picked", align_bytes=64)
         for r in range(2):
-            nc.vector.tensor_copy(q_picked[:, r, :], raw1[r].indirect(query_list[:]))
-
+            nc.scalar.activation(q_picked[:, r, :], raw1[r].indirect(query_list[:]), ACT.Copy)
         nc.scalar.activation(q_grouped[1][:, :, 0:2], q_picked[:].rearrange("p r n -> p n r"), ACT.Copy)
 
-        exp_bias = keep.tile([P, SLOTS // P], F32, name="exp_bias", tag="row_3", align_bytes=64)
+        exp_bias = keep.tile([P, SLOTS // P], F32, name="exp_bias", align_bytes=64)
         lift_bias = keep.tile([P, SLOTS // P], F32, name="lift_bias")
         for b in range(B):
             turned = psum.tile([P, 4, P], F32, name=f"turned_{b}", tag=f"bank_{6 + b}")
@@ -127,7 +127,7 @@ def tile_attend_lq_sgns_topk_kernel(tc, qT, k_words, k_scales, lq, offq, offs, o
             )
 
         q_codes = [
-            keep.tile([P, QUERIES], U32, name="q_codes_0", tag="row_5", align_bytes=64),
+            keep.tile([P, QUERIES], U32, name="q_codes_0", align_bytes=64),
             keep.tile([P, QUERIES], U32, name="q_codes_1", align_bytes=64),
         ]
         quantize(0, 0, QUERIES)

@@ -19,7 +19,7 @@ B, N, T, D, NQ, V = 2, 512, 2048, 1024, 128, 1024
 P = 128
 SLOTS = B * N
 QUERIES = B * NQ
-HALF = V // 2
+LQ_SPLIT = 768
 CHUNK = 256
 KNEE = 20.0
 LIFT = 40.0
@@ -45,7 +45,7 @@ def tile_attend_lq_sgns_topk_kernel(tc, qT, k_words, k_scales, lq, offq, offs, o
 
         lq_pool = keep.tile([P, T], F32, name="lq_pool")
         nc.scalar.dma_start(lq_pool[P - 1 : P, :], lq[0:1, :])
-        nc.gpsimd.memset(lq_pool[0 : P - 1, :], 0.0)
+        nc.vector.memset(lq_pool[0 : P - 1, :], 0.0)
 
         word_pool = keep.tile([P, T], I32, name="word_pool", tag="word_pool", align_bytes=64)
         nc.sync.dma_start(word_pool[:], k_words[0].rearrange("p t b -> p (t b)").bitcast(I32))
@@ -79,7 +79,7 @@ def tile_attend_lq_sgns_topk_kernel(tc, qT, k_words, k_scales, lq, offq, offs, o
         raw1 = load_rows(1, 0, 2, "scale_pool")
 
         lq_row = keep.tile([P, SLOTS], F32, name="lq_row")
-        nc.scalar.activation(lq_row[:, 0:N], lq_pool[:].indirect(slot_list[:, 0 : N // 16]), ACT.Copy)
+        nc.scalar.activation(lq_row[:, 0:LQ_SPLIT], lq_pool[:].indirect(slot_list[:, 0 : LQ_SPLIT // 16]), ACT.Copy)
 
         word_pairs = keep.tile([P, SLOTS], U32, name="word_pairs")
         nc.vector.tensor_copy(word_pairs[:], word_pool[:].bitcast(U32).indirect(slot_list[:]))
@@ -89,35 +89,18 @@ def tile_attend_lq_sgns_topk_kernel(tc, qT, k_words, k_scales, lq, offq, offs, o
         k_codes = keep.tile([P, 2, SLOTS], U16, name="k_codes", align_bytes=64)
         word_halves = word_pairs[:].bitcast(U16).rearrange("p (n o) -> p o n", o=2)
         nc.vector.tensor_copy(k_codes[:], word_halves)
-        nc.vector.tensor_copy(lq_row[:, N:SLOTS], lq_pool[:].indirect(slot_list[:, N // 16 : SLOTS // 16]))
+        nc.vector.tensor_copy(lq_row[:, LQ_SPLIT:SLOTS], lq_pool[:].indirect(slot_list[:, LQ_SPLIT // 16 : SLOTS // 16]))
 
-        q_grouped = [keep.tile([P, QUERIES, 4], BF16, name=f"q_grouped_{o}", align_bytes=64) for o in range(2)]
+        q_grouped = [keep.tile([P, QUERIES, 4], BF16, name="q_grouped_0", tag="q_grouped", align_bytes=64)]
         q_scales = [keep.tile([P, QUERIES], U8, name=f"q_scales_{o}", align_bytes=64) for o in range(2)]
 
-        picked0 = keep.tile([P, 4, QUERIES], F32, name="picked0", align_bytes=64)
-        for r in range(4):
+        picked0 = keep.tile([P, 4, QUERIES], F32, name="picked0", tag="picked", align_bytes=64)
+        for r in range(3):
             nc.scalar.activation(picked0[:, r, :], raw0[r].indirect(query_list[:]), ACT.Copy)
+        nc.vector.tensor_copy(picked0[:, 3, :], raw0[3].indirect(query_list[:]))
         raw1 = raw1 + load_rows(1, 3, 4, "first_rows")
         lay_plane(1, "second_rows")
         nc.vector.tensor_copy(q_grouped[0][:], picked0[:].rearrange("p r n -> p n r"))
-
-        q_picked = keep.tile([P, 2, QUERIES], F32, name="q_picked", align_bytes=64)
-        for r in range(2):
-            nc.scalar.activation(q_picked[:, r, :], raw1[r].indirect(query_list[:]), ACT.Copy)
-        nc.scalar.activation(q_grouped[1][:, :, 0:2], q_picked[:].rearrange("p r n -> p n r"), ACT.Copy)
-
-        exp_bias = keep.tile([P, SLOTS // P], F32, name="exp_bias", align_bytes=64)
-        lift_bias = keep.tile([P, SLOTS // P], F32, name="lift_bias")
-        for b in range(B):
-            turned = psum.tile([P, 4, P], F32, name=f"turned_{b}", tag=f"bank_{6 + b}")
-            for j in range(4):
-                c = 4 * b + j
-                nc.tensor.transpose(turned[:, j, :], lq_row[:, c * P : (c + 1) * P], ident[:])
-            nc.scalar.activation(exp_bias[:, 4 * b : 4 * b + 4], turned[:, :, P - 1], ACT.Copy, scale=-1.0, bias=-math.log(SHRINK))
-        nc.scalar.activation(lift_bias[:], exp_bias[:], ACT.Copy, bias=math.log(SHRINK) + LIFT)
-
-        def gather_row(r, lo, hi):
-            nc.vector.tensor_copy(q_grouped[1][:, lo:hi, r], raw1[r].indirect(query_list[:, lo // 16 : hi // 16]))
 
         def quantize(o, lo, hi):
             nc.vector.quantize_mx(
@@ -131,6 +114,26 @@ def tile_attend_lq_sgns_topk_kernel(tc, qT, k_words, k_scales, lq, offq, offs, o
             keep.tile([P, QUERIES], U32, name="q_codes_1", align_bytes=64),
         ]
         quantize(0, 0, QUERIES)
+
+        exp_bias = keep.tile([P, SLOTS // P], F32, name="exp_bias", align_bytes=64)
+        lift_bias = keep.tile([P, SLOTS // P], F32, name="lift_bias")
+        for b in range(B):
+            turned = psum.tile([P, 4, P], F32, name=f"turned_{b}", tag=f"bank_{6 + b}")
+            for j in range(4):
+                c = 4 * b + j
+                nc.tensor.transpose(turned[:, j, :], lq_row[:, c * P : (c + 1) * P], ident[:])
+            nc.scalar.activation(exp_bias[:, 4 * b : 4 * b + 4], turned[:, :, P - 1], ACT.Copy, scale=-1.0, bias=-math.log(SHRINK))
+        nc.scalar.activation(lift_bias[:], exp_bias[:], ACT.Copy, bias=math.log(SHRINK) + LIFT)
+
+        q_grouped.append(keep.tile([P, QUERIES, 4], BF16, name="q_grouped_1", tag="q_grouped", align_bytes=64))
+        q_picked = keep.tile([P, 2, QUERIES], F32, name="q_picked", tag="picked", align_bytes=64)
+        nc.scalar.activation(q_picked[:, 0, :], raw1[0].indirect(query_list[:]), ACT.Copy)
+        nc.vector.tensor_copy(q_picked[:, 1, :], raw1[1].indirect(query_list[:]))
+        nc.scalar.activation(q_grouped[1][:, :, 0:2], q_picked[:].rearrange("p r n -> p n r"), ACT.Copy)
+
+        def gather_row(r, lo, hi):
+            nc.vector.tensor_copy(q_grouped[1][:, lo:hi, r], raw1[r].indirect(query_list[:, lo // 16 : hi // 16]))
+
         gather_row(2, 0, QUERIES)
         for b in range(B):
             gather_row(3, b * NQ, (b + 1) * NQ)

@@ -19,7 +19,6 @@ B, N, T, D, NQ, V = 2, 512, 2048, 1024, 128, 1024
 P = 128
 SLOTS = B * N
 QUERIES = B * NQ
-LQ_SPLIT = 768
 CHUNK = 256
 KNEE = 20.0
 LIFT = 40.0
@@ -41,7 +40,7 @@ def tile_attend_lq_sgns_topk_kernel(tc, qT, k_words, k_scales, lq, offq, offs, o
         nc.vector.memset(scale_pool[32:64, :], 0)
         nc.vector.memset(scale_pool[64:128, :], 0)
         scale_rows = k_scales.rearrange("o f t -> (o f) t").bitcast(I32)
-        nc.scalar.dma_start(scale_pool[0:32, :], scale_rows)
+        nc.sync.dma_start(scale_pool[0:32, :], scale_rows)
 
         lq_pool = keep.tile([P, T], F32, name="lq_pool")
         nc.scalar.dma_start(lq_pool[P - 1 : P, :], lq[0:1, :])
@@ -79,7 +78,7 @@ def tile_attend_lq_sgns_topk_kernel(tc, qT, k_words, k_scales, lq, offq, offs, o
         raw1 = load_rows(1, 0, 2, "scale_pool")
 
         lq_row = keep.tile([P, SLOTS], F32, name="lq_row")
-        nc.scalar.activation(lq_row[:, 0:LQ_SPLIT], lq_pool[:].indirect(slot_list[:, 0 : LQ_SPLIT // 16]), ACT.Copy)
+        nc.scalar.activation(lq_row[:], lq_pool[:].indirect(slot_list[:]), ACT.Copy)
 
         word_pairs = keep.tile([P, SLOTS], U32, name="word_pairs")
         nc.vector.tensor_copy(word_pairs[:], word_pool[:].bitcast(U32).indirect(slot_list[:]))
@@ -89,7 +88,6 @@ def tile_attend_lq_sgns_topk_kernel(tc, qT, k_words, k_scales, lq, offq, offs, o
         k_codes = keep.tile([P, 2, SLOTS], U16, name="k_codes", align_bytes=64)
         word_halves = word_pairs[:].bitcast(U16).rearrange("p (n o) -> p o n", o=2)
         nc.vector.tensor_copy(k_codes[:], word_halves)
-        nc.vector.tensor_copy(lq_row[:, LQ_SPLIT:SLOTS], lq_pool[:].indirect(slot_list[:, LQ_SPLIT // 16 : SLOTS // 16]))
 
         q_grouped = [keep.tile([P, QUERIES, 4], BF16, name="q_grouped_0", tag="q_grouped", align_bytes=64)]
         q_scales = [keep.tile([P, QUERIES], U8, name=f"q_scales_{o}", align_bytes=64) for o in range(2)]
@@ -127,9 +125,11 @@ def tile_attend_lq_sgns_topk_kernel(tc, qT, k_words, k_scales, lq, offq, offs, o
 
         q_grouped.append(keep.tile([P, QUERIES, 4], BF16, name="q_grouped_1", tag="q_grouped", align_bytes=64))
         q_picked = keep.tile([P, 2, QUERIES], F32, name="q_picked", tag="picked", align_bytes=64)
-        nc.scalar.activation(q_picked[:, 0, :], raw1[0].indirect(query_list[:]), ACT.Copy)
-        nc.vector.tensor_copy(q_picked[:, 1, :], raw1[1].indirect(query_list[:]))
-        nc.scalar.activation(q_grouped[1][:, :, 0:2], q_picked[:].rearrange("p r n -> p n r"), ACT.Copy)
+        for r in range(2):
+            nc.scalar.activation(q_picked[:, r, :], raw1[r].indirect(query_list[:]), ACT.Copy)
+        for b in range(B):
+            cols = slice(b * NQ, (b + 1) * NQ)
+            nc.scalar.activation(q_grouped[1][:, cols, 0:2], q_picked[:, :, cols].rearrange("p r n -> p n r"), ACT.Copy)
 
         def gather_row(r, lo, hi):
             nc.vector.tensor_copy(q_grouped[1][:, lo:hi, r], raw1[r].indirect(query_list[:, lo // 16 : hi // 16]))

@@ -19,7 +19,8 @@ B, N, T, D, NQ, V = 2, 512, 2048, 1024, 128, 1024
 P = 128
 SLOTS = B * N
 QUERIES = B * NQ
-CHUNK = 256
+CHUNKS = SLOTS // P
+CLAMP_WIDTH = 256
 KNEE = 20.0
 LIFT = 40.0
 SHRINK = math.exp(KNEE) / (KNEE + LIFT)
@@ -31,19 +32,19 @@ def tile_attend_lq_sgns_topk_kernel(tc, qT, k_words, k_scales, lq, offq, offs, o
     nc = tc.nc
     with ExitStack() as ctx:
         keep = ctx.enter_context(tc.tile_pool(name="keep", bufs=1))
+        laid = ctx.enter_context(tc.tile_pool(name="laid", bufs=1))
         psum = ctx.enter_context(tc.psum_pool(name="psum", bufs=1))
 
         slot_list = keep.tile([P, SLOTS // 16], U16, name="slot_list")
         nc.sync.dma_start(slot_list[:], offs)
 
-        scale_pool = keep.tile([P, T // 4], I32, name="scale_pool", tag="scale_pool", align_bytes=64)
-        nc.vector.memset(scale_pool[32:64, :], 0)
-        nc.vector.memset(scale_pool[64:128, :], 0)
-        scale_rows = k_scales.rearrange("o f t -> (o f) t").bitcast(I32)
-        nc.sync.dma_start(scale_pool[0:32, :], scale_rows)
-
         lq_pool = keep.tile([P, T], F32, name="lq_pool")
         nc.scalar.dma_start(lq_pool[P - 1 : P, :], lq[0:1, :])
+
+        scale_pool = laid.tile([P, T // 4], I32, name="scale_pool", offset=3072)
+        nc.vector.memset(scale_pool[32:64, :], 0)
+        nc.vector.memset(scale_pool[64:128, :], 0)
+        nc.sync.dma_start(scale_pool[0:32, :], k_scales.rearrange("o f t -> (o f) t").bitcast(I32))
         nc.vector.memset(lq_pool[0 : P - 1, :], 0.0)
 
         word_pool = keep.tile([P, T], I32, name="word_pool", tag="word_pool", align_bytes=64)
@@ -57,64 +58,65 @@ def tile_attend_lq_sgns_topk_kernel(tc, qT, k_words, k_scales, lq, offq, offs, o
 
         q_rows = qT.rearrange("(o p r) n -> o p r n", o=2, r=4)
 
-        def load_rows(o, lo, hi, tag):
-            raw = keep.tile([P, hi - lo, V], F32, name=f"raw_{o}_{lo}", tag=tag, align_bytes=64)
+        def load_rows(raw, o, lo, hi):
             nc.sync.dma_start(raw[:], q_rows[o, :, lo:hi, :])
             return [raw[:, r, :] for r in range(hi - lo)]
 
-        raw0 = load_rows(0, 0, 2, "first_rows") + load_rows(0, 2, 4, "second_rows")
+        rows = [None, None]
+        rows[0] = load_rows(keep.tile([P, 2, V], F32, name="rows_01", align_bytes=64), 0, 0, 2)
+        rows[0] = rows[0] + load_rows(keep.tile([P, 2, V], F32, name="rows_23", tag="second_rows", align_bytes=64), 0, 2, 4)
 
         scale_picked = keep.tile([P, SLOTS], U8, name="scale_picked", align_bytes=64)
         nc.vector.tensor_copy(scale_picked[:], scale_pool[:].bitcast(U8).indirect(slot_list[:]))
-        k_planes = []
 
         def lay_plane(o, tag):
-            k_planes.append(keep.tile([P, SLOTS // 4], I32, name=f"k_plane_{o}", tag=tag, align_bytes=64))
-            for quad in (0, 2, 1, 3):
-                row = 16 * o + 4 * quad
-                nc.sync.dma_start(k_planes[o][32 * quad : 32 * quad + 4, :], scale_picked[row : row + 4, :].bitcast(I32))
+            plane = keep.tile([P, SLOTS // 4], I32, name=f"k_plane_{o}", tag=tag, align_bytes=64)
+            for j in range(4):
+                first = 16 * o + j
+                nc.sync.dma_start(plane[j:P:32, :], scale_picked[first : first + 13 : 4, :].bitcast(I32))
+            return plane[:].bitcast(U8)
 
-        lay_plane(0, "first_plane")
-        raw1 = load_rows(1, 0, 2, "scale_pool")
+        k_scale = [lay_plane(0, "first_plane")]
+        rows[1] = load_rows(laid.tile([P, 2, V], F32, name="rows_45", offset=4096), 1, 0, 2)
 
         lq_row = keep.tile([P, SLOTS], F32, name="lq_row")
         nc.scalar.activation(lq_row[:], lq_pool[:].indirect(slot_list[:]), ACT.Copy)
 
-        word_pairs = keep.tile([P, SLOTS], U32, name="word_pairs")
+        word_pairs = laid.tile([P, SLOTS], U32, name="word_pairs", offset=0)
         nc.vector.tensor_copy(word_pairs[:], word_pool[:].bitcast(U32).indirect(slot_list[:]))
-
-        raw1 = raw1 + load_rows(1, 2, 3, "word_pool")
+        rows[1] = rows[1] + load_rows(keep.tile([P, 1, V], F32, name="rows_6", tag="word_pool", align_bytes=64), 1, 2, 3)
 
         k_codes = keep.tile([P, 2, SLOTS], U16, name="k_codes", align_bytes=64)
-        word_halves = word_pairs[:].bitcast(U16).rearrange("p (n o) -> p o n", o=2)
-        nc.vector.tensor_copy(k_codes[:], word_halves)
+        nc.vector.tensor_copy(k_codes[:], word_pairs[:].bitcast(U16).rearrange("p (n o) -> p o n", o=2))
 
-        q_grouped = [keep.tile([P, QUERIES, 4], BF16, name="q_grouped_0", tag="q_grouped", align_bytes=64)]
+        rows[1] = rows[1] + load_rows(laid.tile([P, 1, V], F32, name="rows_7", offset=0), 1, 3, 4)
+
+        grouped = [[keep.tile([P, NQ, 4], BF16, name=f"grouped_{o}_{b}", align_bytes=64) for b in range(B)] for o in range(2)]
+        picked = [[keep.tile([P, 2, NQ], F32, name=f"picked_{o}_{h}") for h in range(2)] for o in range(2)]
+        q_codes = [keep.tile([P, QUERIES], U32, name=f"q_codes_{o}", align_bytes=64) for o in range(2)]
         q_scales = [keep.tile([P, QUERIES], U8, name=f"q_scales_{o}", align_bytes=64) for o in range(2)]
+        lists = [query_list[:, b * NQ // 16 : (b + 1) * NQ // 16] for b in range(B)]
 
-        picked0 = keep.tile([P, 4, QUERIES], F32, name="picked0", tag="picked", align_bytes=64)
-        for r in range(3):
-            nc.scalar.activation(picked0[:, r, :], raw0[r].indirect(query_list[:]), ACT.Copy)
-        nc.vector.tensor_copy(picked0[:, 3, :], raw0[3].indirect(query_list[:]))
-        raw1 = raw1 + load_rows(1, 3, 4, "first_rows")
-        lay_plane(1, "second_rows")
-        nc.vector.tensor_copy(q_grouped[0][:], picked0[:].rearrange("p r n -> p n r"))
+        def gather_row(o, r):
+            nc.vector.tensor_copy(grouped[o][0][:, :, r], rows[o][r].indirect(lists[0]))
+            nc.scalar.activation(picked[o][r // 2][:, r % 2, :], rows[o][r].indirect(lists[1]), ACT.Copy)
+            if r % 2 == 1:
+                nc.scalar.activation(grouped[o][1][:, :, r - 1 : r + 1], picked[o][r // 2][:].rearrange("p r n -> p n r"), ACT.Copy)
 
-        def quantize(o, lo, hi):
-            nc.vector.quantize_mx(
-                q_codes[o][:, lo:hi].bitcast(FP8X4),
-                q_scales[o][:, lo:hi],
-                q_grouped[o][:, lo:hi, :].rearrange("p n r -> p (n r)"),
-            )
+        def quantize(o, b):
+            cols = slice(b * NQ, (b + 1) * NQ)
+            nc.vector.quantize_mx(q_codes[o][:, cols].bitcast(FP8X4), q_scales[o][:, cols], grouped[o][b][:].rearrange("p n r -> p (n r)"))
 
-        q_codes = [
-            keep.tile([P, QUERIES], U32, name="q_codes_0", align_bytes=64),
-            keep.tile([P, QUERIES], U32, name="q_codes_1", align_bytes=64),
-        ]
-        quantize(0, 0, QUERIES)
+        gather_row(0, 0)
+        gather_row(0, 1)
+        gather_row(0, 2)
+        gather_row(0, 3)
+        k_scale.append(lay_plane(1, "second_rows"))
+        for b in range(B):
+            quantize(0, b)
 
-        exp_bias = keep.tile([P, SLOTS // P], F32, name="exp_bias", align_bytes=64)
-        lift_bias = keep.tile([P, SLOTS // P], F32, name="lift_bias")
+        exp_bias = keep.tile([P, CHUNKS], F32, name="exp_bias", align_bytes=64)
+        lift_bias = keep.tile([P, CHUNKS], F32, name="lift_bias")
         for b in range(B):
             turned = psum.tile([P, 4, P], F32, name=f"turned_{b}", tag=f"bank_{6 + b}")
             for j in range(4):
@@ -123,27 +125,14 @@ def tile_attend_lq_sgns_topk_kernel(tc, qT, k_words, k_scales, lq, offq, offs, o
             nc.scalar.activation(exp_bias[:, 4 * b : 4 * b + 4], turned[:, :, P - 1], ACT.Copy, scale=-1.0, bias=-math.log(SHRINK))
         nc.scalar.activation(lift_bias[:], exp_bias[:], ACT.Copy, bias=math.log(SHRINK) + LIFT)
 
-        q_grouped.append(keep.tile([P, QUERIES, 4], BF16, name="q_grouped_1", tag="q_grouped", align_bytes=64))
-        q_picked = keep.tile([P, 2, QUERIES], F32, name="q_picked", tag="picked", align_bytes=64)
-        for r in range(2):
-            nc.scalar.activation(q_picked[:, r, :], raw1[r].indirect(query_list[:]), ACT.Copy)
+        for r in range(4):
+            gather_row(1, r)
         for b in range(B):
-            cols = slice(b * NQ, (b + 1) * NQ)
-            nc.scalar.activation(q_grouped[1][:, cols, 0:2], q_picked[:, :, cols].rearrange("p r n -> p n r"), ACT.Copy)
+            quantize(1, b)
 
-        def gather_row(r, lo, hi):
-            nc.vector.tensor_copy(q_grouped[1][:, lo:hi, r], raw1[r].indirect(query_list[:, lo // 16 : hi // 16]))
-
-        gather_row(2, 0, QUERIES)
-        for b in range(B):
-            gather_row(3, b * NQ, (b + 1) * NQ)
-        for b in range(B):
-            quantize(1, b * NQ, (b + 1) * NQ)
-
-        k_scale = [plane[:].bitcast(U8) for plane in k_planes]
-        scores = [psum.tile([P, P], F32, name=f"scores_{c}", tag=f"bank_{c}") for c in range(SLOTS // P)]
+        scores = [psum.tile([P, P], F32, name=f"scores_{c}", tag=f"bank_{c}") for c in range(CHUNKS)]
         for o in range(2):
-            for c in range(SLOTS // P):
+            for c in range(CHUNKS):
                 b = c * P // N
                 nc.tensor.matmul_mx(
                     scores[c][:],
@@ -161,13 +150,13 @@ def tile_attend_lq_sgns_topk_kernel(tc, qT, k_words, k_scales, lq, offq, offs, o
         logs = keep.tile([P, SLOTS], F32, name="logs")
         result = keep.tile([P, SLOTS], F32, name="result")
         backs = []
-        for c in range(SLOTS // P):
+        for c in range(CHUNKS):
             cols = slice(c * P, (c + 1) * P)
             nc.scalar.activation(grown[:, cols], scores[c][:], ACT.Exp, bias=exp_bias[:, c : c + 1])
             nc.vector.scalar_tensor_tensor(lesser[:, cols], scores[c][:], lift_bias[:, c : c + 1], grown[:, cols], ALU.add, ALU.min)
-        for lo in range(0, SLOTS, CHUNK):
-            nc.vector.tensor_scalar_max(folded[:, lo : lo + CHUNK], lesser[:, lo : lo + CHUNK], 0.0)
-        for c in range(SLOTS // P):
+        for lo in range(0, SLOTS, CLAMP_WIDTH):
+            nc.vector.tensor_scalar_max(folded[:, lo : lo + CLAMP_WIDTH], lesser[:, lo : lo + CLAMP_WIDTH], 0.0)
+        for c in range(CHUNKS):
             backs.append(psum.tile([P, P], F32, name=f"back_{c}", tag=f"bank_{c}"))
             nc.tensor.transpose(backs[c][:], folded[:, c * P : (c + 1) * P], ident[:])
         for first, last in ((0, 1), (1, 2), (2, 4), (4, 6), (6, 8)):

@@ -63,7 +63,7 @@ def tile_attend_lq_sgns_topk_kernel(tc, qT, k_words, k_scales, lq, offq, offs, o
             return [raw[:, r, :] for r in range(hi - lo)]
 
         rows = [None, None]
-        rows[0] = load_rows(keep.tile([P, 2, V], F32, name="rows_01", align_bytes=64), 0, 0, 2)
+        rows[0] = load_rows(keep.tile([P, 2, V], F32, name="rows_01", tag="first_rows", align_bytes=64), 0, 0, 2)
         rows[0] = rows[0] + load_rows(keep.tile([P, 2, V], F32, name="rows_23", tag="second_rows", align_bytes=64), 0, 2, 4)
 
         scale_picked = keep.tile([P, SLOTS], U8, name="scale_picked", align_bytes=64)
@@ -89,31 +89,22 @@ def tile_attend_lq_sgns_topk_kernel(tc, qT, k_words, k_scales, lq, offq, offs, o
         k_codes = keep.tile([P, 2, SLOTS], U16, name="k_codes", align_bytes=64)
         nc.vector.tensor_copy(k_codes[:], word_pairs[:].bitcast(U16).rearrange("p (n o) -> p o n", o=2))
 
-        rows[1] = rows[1] + load_rows(laid.tile([P, 1, V], F32, name="rows_7", offset=0), 1, 3, 4)
-
-        grouped = [[keep.tile([P, NQ, 4], BF16, name=f"grouped_{o}_{b}", align_bytes=64) for b in range(B)] for o in range(2)]
-        picked = [[keep.tile([P, 2, NQ], F32, name=f"picked_{o}_{h}") for h in range(2)] for o in range(2)]
+        grouped_0 = keep.tile([P, QUERIES, 4], BF16, name="grouped_0", align_bytes=64)
+        grouped_1 = [keep.tile([P, NQ, 4], BF16, name=f"grouped_1_{b}", align_bytes=64) for b in range(B)]
         q_codes = [keep.tile([P, QUERIES], U32, name=f"q_codes_{o}", align_bytes=64) for o in range(2)]
         q_scales = [keep.tile([P, QUERIES], U8, name=f"q_scales_{o}", align_bytes=64) for o in range(2)]
         lists = [query_list[:, b * NQ // 16 : (b + 1) * NQ // 16] for b in range(B)]
 
-        def gather_row(o, r):
-            nc.vector.tensor_copy(grouped[o][0][:, :, r], rows[o][r].indirect(lists[0]))
-            nc.scalar.activation(picked[o][r // 2][:, r % 2, :], rows[o][r].indirect(lists[1]), ACT.Copy)
-            if r % 2 == 1:
-                nc.scalar.activation(grouped[o][1][:, :, r - 1 : r + 1], picked[o][r // 2][:].rearrange("p r n -> p n r"), ACT.Copy)
+        def quantize(o, lo, hi, grouped):
+            nc.vector.quantize_mx(q_codes[o][:, lo:hi].bitcast(FP8X4), q_scales[o][:, lo:hi], grouped[:].rearrange("p n r -> p (n r)"))
 
-        def quantize(o, b):
-            cols = slice(b * NQ, (b + 1) * NQ)
-            nc.vector.quantize_mx(q_codes[o][:, cols].bitcast(FP8X4), q_scales[o][:, cols], grouped[o][b][:].rearrange("p n r -> p (n r)"))
-
-        gather_row(0, 0)
-        gather_row(0, 1)
-        gather_row(0, 2)
-        gather_row(0, 3)
+        picked_0 = keep.tile([P, 4, QUERIES], F32, name="picked_0")
+        for r in range(4):
+            nc.scalar.activation(picked_0[:, r, :], rows[0][r].indirect(query_list[:]), ACT.Copy)
+        rows[1] = rows[1] + load_rows(keep.tile([P, 1, V], F32, name="rows_7", tag="first_rows", align_bytes=64), 1, 3, 4)
         k_scale.append(lay_plane(1, "second_rows"))
-        for b in range(B):
-            quantize(0, b)
+        nc.vector.tensor_copy(grouped_0[:], picked_0[:].rearrange("p r n -> p n r"))
+        quantize(0, 0, QUERIES, grouped_0)
 
         exp_bias = keep.tile([P, CHUNKS], F32, name="exp_bias", align_bytes=64)
         lift_bias = keep.tile([P, CHUNKS], F32, name="lift_bias")
@@ -125,10 +116,18 @@ def tile_attend_lq_sgns_topk_kernel(tc, qT, k_words, k_scales, lq, offq, offs, o
             nc.scalar.activation(exp_bias[:, 4 * b : 4 * b + 4], turned[:, :, P - 1], ACT.Copy, scale=-1.0, bias=-math.log(SHRINK))
         nc.scalar.activation(lift_bias[:], exp_bias[:], ACT.Copy, bias=math.log(SHRINK) + LIFT)
 
-        for r in range(4):
-            gather_row(1, r)
+        picked_1 = keep.tile([P, 2, QUERIES], F32, name="picked_1")
+        for r in range(2):
+            nc.scalar.activation(picked_1[:, r, :], rows[1][r].indirect(query_list[:]), ACT.Copy)
         for b in range(B):
-            quantize(1, b)
+            nc.scalar.activation(grouped_1[b][:, :, 0:2], picked_1[:, :, b * NQ : (b + 1) * NQ].rearrange("p r n -> p n r"), ACT.Copy)
+            nc.vector.tensor_copy(grouped_1[b][:, :, 2], rows[1][2].indirect(lists[b]))
+        last_picked = keep.tile([P, NQ], F32, name="last_picked")
+        nc.scalar.activation(last_picked[:], rows[1][3].indirect(lists[1]), ACT.Copy)
+        nc.vector.tensor_copy(grouped_1[0][:, :, 3], rows[1][3].indirect(lists[0]))
+        quantize(1, 0, NQ, grouped_1[0])
+        nc.vector.tensor_copy(grouped_1[1][:, :, 3], last_picked[:])
+        quantize(1, NQ, QUERIES, grouped_1[1])
 
         scores = [psum.tile([P, P], F32, name=f"scores_{c}", tag=f"bank_{c}") for c in range(CHUNKS)]
         for o in range(2):

@@ -99,8 +99,9 @@ def tile_attend_lq_sgns_topk_kernel(tc, qT, k_words, k_scales, lq, offq, offs, o
             nc.vector.quantize_mx(q_codes[o][:, lo:hi].bitcast(FP8X4), q_scales[o][:, lo:hi], grouped[:].rearrange("p n r -> p (n r)"))
 
         picked_0 = keep.tile([P, 4, QUERIES], F32, name="picked_0")
-        for r in range(4):
+        for r in range(3):
             nc.scalar.activation(picked_0[:, r, :], rows[0][r].indirect(query_list[:]), ACT.Copy)
+        nc.vector.tensor_copy(picked_0[:, 3, :], rows[0][3].indirect(query_list[:]))
         rows[1] = rows[1] + load_rows(keep.tile([P, 1, V], F32, name="rows_7", tag="first_rows", align_bytes=64), 1, 3, 4)
         k_scale.append(lay_plane(1, "second_rows"))
         nc.vector.tensor_copy(grouped_0[:], picked_0[:].rearrange("p r n -> p n r"))
@@ -116,17 +117,14 @@ def tile_attend_lq_sgns_topk_kernel(tc, qT, k_words, k_scales, lq, offq, offs, o
             nc.scalar.activation(exp_bias[:, 4 * b : 4 * b + 4], turned[:, :, P - 1], ACT.Copy, scale=-1.0, bias=-math.log(SHRINK))
         nc.scalar.activation(lift_bias[:], exp_bias[:], ACT.Copy, bias=math.log(SHRINK) + LIFT)
 
-        picked_1 = keep.tile([P, 2, QUERIES], F32, name="picked_1")
-        for r in range(2):
-            nc.scalar.activation(picked_1[:, r, :], rows[1][r].indirect(query_list[:]), ACT.Copy)
-        for b in range(B):
-            nc.scalar.activation(grouped_1[b][:, :, 0:2], picked_1[:, :, b * NQ : (b + 1) * NQ].rearrange("p r n -> p n r"), ACT.Copy)
-            nc.vector.tensor_copy(grouped_1[b][:, :, 2], rows[1][2].indirect(lists[b]))
-        last_picked = keep.tile([P, NQ], F32, name="last_picked")
-        nc.scalar.activation(last_picked[:], rows[1][3].indirect(lists[1]), ACT.Copy)
-        nc.vector.tensor_copy(grouped_1[0][:, :, 3], rows[1][3].indirect(lists[0]))
+        picked_1 = [keep.tile([P, 2, NQ], F32, name=f"picked_1_{h}") for h in range(2)]
+        for r in range(4):
+            nc.vector.tensor_copy(grouped_1[0][:, :, r], rows[1][r].indirect(lists[0]))
+            nc.scalar.activation(picked_1[r // 2][:, r % 2, :], rows[1][r].indirect(lists[1]), ACT.Copy)
+            if r == 1:
+                nc.scalar.activation(grouped_1[1][:, :, 0:2], picked_1[0][:].rearrange("p r n -> p n r"), ACT.Copy)
         quantize(1, 0, NQ, grouped_1[0])
-        nc.vector.tensor_copy(grouped_1[1][:, :, 3], last_picked[:])
+        nc.vector.tensor_copy(grouped_1[1][:, :, 2:4], picked_1[1][:].rearrange("p r n -> p n r"))
         quantize(1, NQ, QUERIES, grouped_1[1])
 
         scores = [psum.tile([P, P], F32, name=f"scores_{c}", tag=f"bank_{c}") for c in range(CHUNKS)]

@@ -35,19 +35,19 @@ def tile_attend_lq_sgns_topk_kernel(tc, qT, k_words, k_scales, lq, offq, offs, o
         laid = ctx.enter_context(tc.tile_pool(name="laid", bufs=1))
         psum = ctx.enter_context(tc.psum_pool(name="psum", bufs=1))
 
-        slot_list = keep.tile([P, SLOTS // 16], U16, name="slot_list")
+        slot_list = keep.tile([P, SLOTS // 16], U16, name="slot_list", align_bytes=256)
         nc.sync.dma_start(slot_list[:], offs)
 
-        lq_pool = keep.tile([P, T], F32, name="lq_pool")
+        lq_pool = keep.tile([P, T], F32, name="lq_pool", align_bytes=256)
         nc.scalar.dma_start(lq_pool[P - 1 : P, :], lq[0:1, :])
 
-        scale_pool = laid.tile([P, T // 4], I32, name="scale_pool", offset=3072)
+        scale_pool = laid.tile([P, T // 4], I32, name="scale_pool", offset=3072, align_bytes=256)
         nc.vector.memset(scale_pool[32:64, :], 0)
         nc.vector.memset(scale_pool[64:128, :], 0)
         nc.sync.dma_start(scale_pool[0:32, :], k_scales.rearrange("o f t -> (o f) t").bitcast(I32))
         nc.vector.memset(lq_pool[0 : P - 1, :], 0.0)
 
-        word_pool = keep.tile([P, T], I32, name="word_pool", tag="word_pool", align_bytes=64)
+        word_pool = keep.tile([P, T], I32, name="word_pool", tag="word_pool", align_bytes=256)
         nc.sync.dma_start(word_pool[:], k_words[0].rearrange("p t b -> p (t b)").bitcast(I32))
 
         query_list = keep.tile([P, QUERIES // 16], U16, name="query_list")
@@ -63,36 +63,36 @@ def tile_attend_lq_sgns_topk_kernel(tc, qT, k_words, k_scales, lq, offq, offs, o
             return [raw[:, r, :] for r in range(hi - lo)]
 
         rows = [None, None]
-        rows[0] = load_rows(keep.tile([P, 2, V], F32, name="rows_01", tag="first_rows", align_bytes=64), 0, 0, 2)
-        rows[0] = rows[0] + load_rows(keep.tile([P, 2, V], F32, name="rows_23", tag="second_rows", align_bytes=64), 0, 2, 4)
+        rows[0] = load_rows(keep.tile([P, 2, V], F32, name="rows_01", tag="first_rows", align_bytes=256), 0, 0, 2)
+        rows[0] = rows[0] + load_rows(keep.tile([P, 2, V], F32, name="rows_23", tag="second_rows", align_bytes=256), 0, 2, 4)
 
-        scale_picked = keep.tile([P, SLOTS], U8, name="scale_picked", align_bytes=64)
+        scale_picked = keep.tile([P, SLOTS], U8, name="scale_picked", align_bytes=256)
         nc.vector.tensor_copy(scale_picked[:], scale_pool[:].bitcast(U8).indirect(slot_list[:]))
 
         def lay_plane(o, tag):
-            plane = keep.tile([P, SLOTS // 4], I32, name=f"k_plane_{o}", tag=tag, align_bytes=64)
+            plane = keep.tile([P, SLOTS // 4], I32, name=f"k_plane_{o}", tag=tag, align_bytes=256)
             for j in range(4):
                 first = 16 * o + j
                 nc.sync.dma_start(plane[j:P:32, :], scale_picked[first : first + 13 : 4, :].bitcast(I32))
             return plane[:].bitcast(U8)
 
         k_scale = [lay_plane(0, "first_plane")]
-        rows[1] = load_rows(laid.tile([P, 2, V], F32, name="rows_45", offset=4096), 1, 0, 2)
+        rows[1] = load_rows(laid.tile([P, 2, V], F32, name="rows_45", offset=4096, align_bytes=256), 1, 0, 2)
 
         lq_row = keep.tile([P, SLOTS], F32, name="lq_row")
         nc.scalar.activation(lq_row[:], lq_pool[:].indirect(slot_list[:]), ACT.Copy)
 
-        word_pairs = laid.tile([P, SLOTS], U32, name="word_pairs", offset=0)
+        word_pairs = laid.tile([P, SLOTS], U32, name="word_pairs", offset=0, align_bytes=256)
         nc.vector.tensor_copy(word_pairs[:], word_pool[:].bitcast(U32).indirect(slot_list[:]))
-        rows[1] = rows[1] + load_rows(keep.tile([P, 1, V], F32, name="rows_6", tag="word_pool", align_bytes=64), 1, 2, 3)
+        rows[1] = rows[1] + load_rows(keep.tile([P, 1, V], F32, name="rows_6", tag="word_pool", align_bytes=256), 1, 2, 3)
 
-        k_codes = keep.tile([P, 2, SLOTS], U16, name="k_codes", align_bytes=64)
+        k_codes = keep.tile([P, 2, SLOTS], U16, name="k_codes", align_bytes=256)
         nc.vector.tensor_copy(k_codes[:], word_pairs[:].bitcast(U16).rearrange("p (n o) -> p o n", o=2))
 
-        grouped_0 = keep.tile([P, QUERIES, 4], BF16, name="grouped_0", align_bytes=64)
-        grouped_1 = [keep.tile([P, NQ, 4], BF16, name=f"grouped_1_{b}", align_bytes=64) for b in range(B)]
-        q_codes = [keep.tile([P, QUERIES], U32, name=f"q_codes_{o}", align_bytes=64) for o in range(2)]
-        q_scales = [keep.tile([P, QUERIES], U8, name=f"q_scales_{o}", align_bytes=64) for o in range(2)]
+        grouped_0 = keep.tile([P, QUERIES, 4], BF16, name="grouped_0", align_bytes=256)
+        grouped_1 = [keep.tile([P, NQ, 4], BF16, name=f"grouped_1_{b}", align_bytes=256) for b in range(B)]
+        q_codes = [keep.tile([P, QUERIES], U32, name=f"q_codes_{o}", align_bytes=256) for o in range(2)]
+        q_scales = [keep.tile([P, QUERIES], U8, name=f"q_scales_{o}", align_bytes=256) for o in range(2)]
         lists = [query_list[:, b * NQ // 16 : (b + 1) * NQ // 16] for b in range(B)]
 
         def quantize(o, lo, hi, grouped):
@@ -102,12 +102,12 @@ def tile_attend_lq_sgns_topk_kernel(tc, qT, k_words, k_scales, lq, offq, offs, o
         for r in range(3):
             nc.scalar.activation(picked_0[:, r, :], rows[0][r].indirect(query_list[:]), ACT.Copy)
         nc.vector.tensor_copy(picked_0[:, 3, :], rows[0][3].indirect(query_list[:]))
-        rows[1] = rows[1] + load_rows(keep.tile([P, 1, V], F32, name="rows_7", tag="first_rows", align_bytes=64), 1, 3, 4)
+        rows[1] = rows[1] + load_rows(keep.tile([P, 1, V], F32, name="rows_7", tag="first_rows", align_bytes=256), 1, 3, 4)
         k_scale.append(lay_plane(1, "second_rows"))
         nc.vector.tensor_copy(grouped_0[:], picked_0[:].rearrange("p r n -> p n r"))
         quantize(0, 0, QUERIES, grouped_0)
 
-        exp_bias = keep.tile([P, CHUNKS], F32, name="exp_bias", align_bytes=64)
+        exp_bias = keep.tile([P, CHUNKS], F32, name="exp_bias", align_bytes=256)
         lift_bias = keep.tile([P, CHUNKS], F32, name="lift_bias")
         for b in range(B):
             turned = psum.tile([P, 4, P], F32, name=f"turned_{b}", tag=f"bank_{6 + b}")
@@ -145,7 +145,7 @@ def tile_attend_lq_sgns_topk_kernel(tc, qT, k_words, k_scales, lq, offq, offs, o
         grown = keep.tile([P, SLOTS], F32, name="grown")
         folded = keep.tile([P, SLOTS], F32, name="folded")
         logs = keep.tile([P, SLOTS], F32, name="logs")
-        result = keep.tile([P, SLOTS], F32, name="result")
+        result = keep.tile([P, SLOTS], F32, name="result", align_bytes=256)
         backs = []
         for c in range(CHUNKS):
             cols = slice(c * P, (c + 1) * P)

import math
from contextlib import ExitStack

import concourse.mybir as mybir
from concourse.masks import make_identity

F32 = mybir.dt.float32
BF16 = mybir.dt.bfloat16
I32 = mybir.dt.int32
U32 = mybir.dt.uint32
U16 = mybir.dt.uint16
U8 = mybir.dt.uint8
FP8X4 = mybir.dt.float8_e4m3fn_x4
FP4X4 = mybir.dt.float4_e2m1fn_x4
ACT = mybir.ActivationFunctionType
ALU = mybir.AluOpType

B, N, T, D, NQ, V = 2, 512, 2048, 1024, 128, 1024
P = 128
SLOTS = B * N
QUERIES = B * NQ
CHUNKS = SLOTS // P
CLAMP_WIDTH = 256
KNEE = 20.0
LIFT = 40.0
SHRINK = math.exp(KNEE) / (KNEE + LIFT)
FLOPS = 2 * B * NQ * N * D
BYTES = 4 * D * V + P * T * 4 + 2 * 16 * T + 4 * T + 2 * P * (16 + 64) + 4 * B * NQ * N


def tile_attend_lq_sgns_topk_kernel(tc, qT, k_words, k_scales, lq, offq, offs, out):
    nc = tc.nc
    with ExitStack() as ctx:
        keep = ctx.enter_context(tc.tile_pool(name="keep", bufs=1))
        laid = ctx.enter_context(tc.tile_pool(name="laid", bufs=1))
        psum = ctx.enter_context(tc.psum_pool(name="psum", bufs=1))

        slot_list = keep.tile([P, SLOTS // 16], U16, name="slot_list", align_bytes=256)
        nc.sync.dma_start(slot_list[:], offs)

        lq_pool = keep.tile([P, T], F32, name="lq_pool", align_bytes=256)
        nc.scalar.dma_start(lq_pool[P - 1 : P, :], lq[0:1, :])

        scale_pool = laid.tile([P, T // 4], I32, name="scale_pool", offset=3072, align_bytes=256)
        nc.vector.memset(scale_pool[32:64, :], 0)
        nc.vector.memset(scale_pool[64:128, :], 0)
        nc.sync.dma_start(scale_pool[0:32, :], k_scales.rearrange("o f t -> (o f) t").bitcast(I32))
        nc.vector.memset(lq_pool[0 : P - 1, :], 0.0)

        word_pool = keep.tile([P, T], I32, name="word_pool", tag="word_pool", align_bytes=256)
        nc.sync.dma_start(word_pool[:], k_words[0].rearrange("p t b -> p (t b)").bitcast(I32))

        query_list = keep.tile([P, QUERIES // 16], U16, name="query_list")
        nc.sync.dma_start(query_list[:], offq)

        ident = keep.tile([P, P], F32, name="ident")
        make_identity(nc, ident[:])

        q_rows = qT.rearrange("(o p r) n -> o p r n", o=2, r=4)

        def load_rows(raw, o, lo, hi):
            nc.sync.dma_start(raw[:], q_rows[o, :, lo:hi, :])
            return [raw[:, r, :] for r in range(hi - lo)]

        rows = [None, None]
        rows[0] = load_rows(keep.tile([P, 2, V], F32, name="rows_01", tag="first_rows", align_bytes=256), 0, 0, 2)
        rows[0] = rows[0] + load_rows(keep.tile([P, 2, V], F32, name="rows_23", tag="second_rows", align_bytes=256), 0, 2, 4)

        scale_picked = keep.tile([P, SLOTS], U8, name="scale_picked", align_bytes=256)
        nc.vector.tensor_copy(scale_picked[:], scale_pool[:].bitcast(U8).indirect(slot_list[:]))

        def lay_plane(o, tag):
            plane = keep.tile([P, SLOTS // 4], I32, name=f"k_plane_{o}", tag=tag, align_bytes=256)
            for j in range(4):
                first = 16 * o + j
                nc.sync.dma_start(plane[j:P:32, :], scale_picked[first : first + 13 : 4, :].bitcast(I32))
            return plane[:].bitcast(U8)

        k_scale = [lay_plane(0, "first_plane")]
        rows[1] = load_rows(laid.tile([P, 2, V], F32, name="rows_45", offset=4096, align_bytes=256), 1, 0, 2)

        lq_row = keep.tile([P, SLOTS], F32, name="lq_row")
        nc.scalar.activation(lq_row[:], lq_pool[:].indirect(slot_list[:]), ACT.Copy)

        word_pairs = laid.tile([P, SLOTS], U32, name="word_pairs", offset=0, align_bytes=256)
        nc.vector.tensor_copy(word_pairs[:], word_pool[:].bitcast(U32).indirect(slot_list[:]))
        rows[1] = rows[1] + load_rows(keep.tile([P, 1, V], F32, name="rows_6", tag="word_pool", align_bytes=256), 1, 2, 3)

        k_codes = keep.tile([P, 2, SLOTS], U16, name="k_codes", align_bytes=256)
        nc.vector.tensor_copy(k_codes[:], word_pairs[:].bitcast(U16).rearrange("p (n o) -> p o n", o=2))

        grouped_0 = keep.tile([P, QUERIES, 4], BF16, name="grouped_0", align_bytes=256)
        grouped_1 = [keep.tile([P, NQ, 4], BF16, name=f"grouped_1_{b}", align_bytes=256) for b in range(B)]
        q_codes = [keep.tile([P, QUERIES], U32, name=f"q_codes_{o}", align_bytes=256) for o in range(2)]
        q_scales = [keep.tile([P, QUERIES], U8, name=f"q_scales_{o}", align_bytes=256) for o in range(2)]
        lists = [query_list[:, b * NQ // 16 : (b + 1) * NQ // 16] for b in range(B)]

        def quantize(o, lo, hi, grouped):
            nc.vector.quantize_mx(q_codes[o][:, lo:hi].bitcast(FP8X4), q_scales[o][:, lo:hi], grouped[:].rearrange("p n r -> p (n r)"))

        picked_0 = keep.tile([P, 4, QUERIES], F32, name="picked_0")
        for r in range(3):
            nc.scalar.activation(picked_0[:, r, :], rows[0][r].indirect(query_list[:]), ACT.Copy)
        nc.vector.tensor_copy(picked_0[:, 3, :], rows[0][3].indirect(query_list[:]))
        rows[1] = rows[1] + load_rows(keep.tile([P, 1, V], F32, name="rows_7", tag="first_rows", align_bytes=256), 1, 3, 4)
        k_scale.append(lay_plane(1, "second_rows"))
        nc.vector.tensor_copy(grouped_0[:], picked_0[:].rearrange("p r n -> p n r"))
        quantize(0, 0, QUERIES, grouped_0)

        exp_bias = keep.tile([P, CHUNKS], F32, name="exp_bias", align_bytes=256)
        lift_bias = keep.tile([P, CHUNKS], F32, name="lift_bias")
        for b in range(B):
            turned = psum.tile([P, 4, P], F32, name=f"turned_{b}", tag=f"bank_{6 + b}")
            for j in range(4):
                c = 4 * b + j
                nc.tensor.transpose(turned[:, j, :], lq_row[:, c * P : (c + 1) * P], ident[:])
            nc.scalar.activation(exp_bias[:, 4 * b : 4 * b + 4], turned[:, :, P - 1], ACT.Copy, scale=-1.0, bias=-math.log(SHRINK))
        nc.scalar.activation(lift_bias[:], exp_bias[:], ACT.Copy, bias=math.log(SHRINK) + LIFT)

        picked_1 = [keep.tile([P, 2, NQ], F32, name=f"picked_1_{h}") for h in range(2)]
        for r in range(4):
            nc.vector.tensor_copy(grouped_1[0][:, :, r], rows[1][r].indirect(lists[0]))
            nc.scalar.activation(picked_1[r // 2][:, r % 2, :], rows[1][r].indirect(lists[1]), ACT.Copy)
            if r == 1:
                nc.scalar.activation(grouped_1[1][:, :, 0:2], picked_1[0][:].rearrange("p r n -> p n r"), ACT.Copy)
        quantize(1, 0, NQ, grouped_1[0])
        nc.vector.tensor_copy(grouped_1[1][:, :, 2:4], picked_1[1][:].rearrange("p r n -> p n r"))
        quantize(1, NQ, QUERIES, grouped_1[1])

        scores = [psum.tile([P, P], F32, name=f"scores_{c}", tag=f"bank_{c}") for c in range(CHUNKS)]
        for o in range(2):
            for c in range(CHUNKS):
                b = c * P // N
                nc.tensor.matmul_mx(
                    scores[c][:],
                    lhsT=k_codes[:, o, c * P : (c + 1) * P].bitcast(FP4X4),
                    lhsT_scale=k_scale[o][:, c * P : (c + 1) * P],
                    rhs=q_codes[o][:, b * NQ : (b + 1) * NQ].bitcast(FP8X4),
                    rhs_scale=q_scales[o][:, b * NQ : (b + 1) * NQ],
                    start=(o == 0),
                    stop=(o == 1),
                )

        lesser = keep.tile([P, SLOTS], F32, name="lesser")
        grown = keep.tile([P, SLOTS], F32, name="grown")
        folded = keep.tile([P, SLOTS], F32, name="folded")
        logs = keep.tile([P, SLOTS], F32, name="logs")
        result = keep.tile([P, SLOTS], F32, name="result", align_bytes=256)
        backs = []
        for c in range(CHUNKS):
            cols = slice(c * P, (c + 1) * P)
            nc.scalar.activation(grown[:, cols], scores[c][:], ACT.Exp, bias=exp_bias[:, c : c + 1])
            nc.vector.scalar_tensor_tensor(lesser[:, cols], scores[c][:], lift_bias[:, c : c + 1], grown[:, cols], ALU.add, ALU.min)
        for lo in range(0, SLOTS, CLAMP_WIDTH):
            nc.vector.tensor_scalar_max(folded[:, lo : lo + CLAMP_WIDTH], lesser[:, lo : lo + CLAMP_WIDTH], 0.0)
        for c in range(CHUNKS):
            backs.append(psum.tile([P, P], F32, name=f"back_{c}", tag=f"bank_{c}"))
            nc.tensor.transpose(backs[c][:], folded[:, c * P : (c + 1) * P], ident[:])
        for first, last in ((0, 1), (1, 2), (2, 4), (4, 6), (6, 8)):
            for c in range(first, last):
                cols = slice(c * P, (c + 1) * P)
                nc.scalar.activation(logs[:, cols], backs[c][:], ACT.Ln, bias=1.0, scale=SHRINK)
                nc.vector.scalar_tensor_tensor(result[:, cols], backs[c][:], -LIFT, logs[:, cols], ALU.add, ALU.max)
            lo, hi = first * P, last * P
            nc.sync.dma_start(out[lo // N, :, lo % N : lo % N + hi - lo], result[:, lo:hi])
